import numpy as np
import ml_dtypes


def mxq(x, axis, fmt="e4m3"):
    dtype, down = {"e4m3": (ml_dtypes.float8_e4m3fn, 7), "e5m2": (ml_dtypes.float8_e5m2, 14)}[fmt]
    v = np.moveaxis(np.asarray(x, np.float32).astype(ml_dtypes.bfloat16).astype(np.float64), axis, -1)
    blocks = v.reshape(v.shape[:-1] + (-1, 32))
    amax = np.abs(blocks).max(-1, keepdims=True)
    byte = np.maximum(np.where(amax > 0, np.frexp(amax)[1] - 1 + 127, 0) - down, 1)
    scale = np.exp2(byte - 127.0)
    codes = (blocks / scale).astype(np.float32).astype(dtype).astype(np.float64)
    return np.moveaxis((codes * scale).reshape(v.shape), -1, axis)


WIDE = False


def mx_kscale(k):
    if not WIDE:
        return np.ones(k)
    levels = np.array([18, -18])
    if k % 512:
        return np.exp2(np.random.permutation(np.resize(levels, k // 32))).repeat(32)
    a = np.empty((k // 512, 16))
    for p in range(k // 512):
        a[p, :8] = np.random.permutation(np.resize(levels, 8))
        for g in range(8):
            far = levels[np.abs(levels - a[p, g]) >= 10]
            a[p, g + 8] = far[np.random.randint(len(far))]
    return np.exp2(a.ravel()).repeat(32)


def f64(x):
    return np.asarray(x).astype(np.float64)


def striped(idx):
    return np.tile(np.asarray(idx).reshape(-1, 16).T, (8, 1)).astype(np.uint16)


def unstriped(offs):
    return offs[:16].T.reshape(-1).astype(np.int64)

def planes(y):
    n, m = y.shape
    v = y.astype(np.float32).astype(ml_dtypes.bfloat16).astype(np.float64).reshape(n // 32, 32, m)
    top = np.abs(v).max(1)
    byte = np.clip(np.where(top > 0, np.frexp(top)[1] - 1 + 127 - 7, 1), 1, 254)
    codes = (v * np.exp2(127.0 - byte)[:, None, :]).reshape(n, m).astype(np.float32).astype(ml_dtypes.float8_e4m3fn).view(np.uint8)
    words = codes.reshape(n // 512, 128, 4, m).transpose(0, 1, 3, 2)
    return np.ascontiguousarray(words), np.ascontiguousarray(byte.astype(np.uint8).reshape(n // 512, 16, m))


T, C, D, DV = 512, 1024, 512, 1024
BETA = 0.25


def setup_inputs():
    n = np.random.standard_normal
    grid = lambda v: np.clip(np.round(v * 16) / 16, -4, 4)
    v = mx_kscale(DV)[:, None]
    return {
        "zT": (grid(n((DV, T))) * v).astype(np.float32),
        "cb": (grid(n((DV, C))) * v).astype(np.float32),
        "dyT": (grid(0.5 * n((DV, T))) * v).astype(np.float32),
        "wm": (n((DV, D)) / np.sqrt(DV) / v).astype(np.float32),
        "offs": striped(np.random.randint(0, C, T)),
    }


def reference(zT, cb, dyT, wm, offs):
    e = f64(zT) - f64(cb)[:, unstriped(offs)]
    g = (f64(dyT) + BETA * e)
    out_0 = mxq(f64(wm), 0, "e4m3").T @ mxq(g, 0, "e5m2")
    return (out_0,) + planes(out_0)

@@ -1,0 +1,161 @@
+from contextlib import ExitStack
+
+import concourse.mybir as mybir
+
+T, C, D, DV = 512, 1024, 512, 1024
+BETA = 0.25
+FLOPS = 2 * DV * D * T
+
+F32 = mybir.dt.float32
+BF16 = mybir.dt.bfloat16
+U32 = mybir.dt.uint32
+I32 = mybir.dt.int32
+U16 = mybir.dt.uint16
+U8 = mybir.dt.uint8
+E4M3 = mybir.dt.float8_e4m3fn_x4
+E5M2 = mybir.dt.float8_e5m2_x4
+MULT = mybir.AluOpType.mult
+ADD = mybir.AluOpType.add
+COPY = mybir.ActivationFunctionType.Copy
+
+P = 128
+PACK = 4
+K_PASS = P * PACK
+PASSES = DV // K_PASS
+HALF = 256
+LINE = 4
+
+
+def tile_attend_gvq_pl_s_x_kernel(tc, zT, cb, dyT, wm, offs, out_0, out_1, out_2):
+    nc = tc.nc
+
+    def rows(src, a):
+        return src[a * K_PASS:(a + 1) * K_PASS, :].rearrange("(p k) c -> p k c", k=PACK)
+
+    with ExitStack() as ctx:
+        held = ctx.enter_context(tc.tile_pool(name="held", bufs=1))
+        sb = ctx.enter_context(tc.tile_pool(name="sb", bufs=1))
+        psum = ctx.enter_context(tc.psum_pool(name="psum", bufs=1))
+
+        offsets = held.tile([P, T // 16], U16, name="offsets")
+        nc.sync.dma_start(offsets[:], offs)
+
+        picked = [sb.tile([P, PACK, T], F32, name=f"picked{a}") for a in range(PASSES)]
+        zs = [sb.tile([P, PACK, T], F32, name=f"zs{a}") for a in range(PASSES)]
+        part = [sb.tile([P, PACK, T], F32, name=f"part{a}") for a in range(PASSES)]
+        g_bf = [sb.tile([P, T, PACK], BF16, name=f"g_bf{a}", align_bytes=64) for a in range(PASSES)]
+        g_codes = [sb.tile([P, T], U32, name=f"g_codes{a}", align_bytes=64) for a in range(PASSES)]
+        g_scales = [sb.tile([P, T], U8, name=f"g_scales{a}", align_bytes=64) for a in range(PASSES)]
+        w_bf = [sb.tile([P, PACK, P, PACK], BF16, name=f"w_bf{a}", align_bytes=64) for a in range(PASSES)]
+        w_codes = [sb.tile([P, D], U32, name=f"w_codes{a}", align_bytes=64) for a in range(PASSES)]
+        w_scales = [sb.tile([P, D], U8, name=f"w_scales{a}", align_bytes=64) for a in range(PASSES)]
+        banks = [psum.tile([P, T], F32, name=f"bank{j}") for j in range(PACK)]
+
+        def look_up(a, k):
+            book = sb.tile([P, C], F32, name=f"book{a}{k}")
+            nc.sync.dma_start(book[:], rows(cb, a)[:, k, :])
+            nc.vector.tensor_copy(picked[a][:, k, :], book[:].indirect(offsets[:]))
+
+        def commitment(a, h):
+            ks = slice(2 * h, 2 * h + 2)
+            z = sb.tile([P, 2, T], F32, name=f"z{a}{h}")
+            nc.sync.dma_start(z[:], rows(zT, a)[:, ks, :])
+            nc.scalar.activation(zs[a][:, ks, :], z[:], COPY, scale=BETA)
+            nc.vector.scalar_tensor_tensor(part[a][:, ks, :], picked[a][:, ks, :], -BETA, zs[a][:, ks, :], MULT, ADD)
+
+        def gradient(a, t0, width):
+            ts = slice(t0, t0 + width)
+            dy = sb.tile([P, PACK, width], F32, name=f"dy{a}{t0}")
+            nc.sync.dma_start(dy[:], rows(dyT, a)[:, :, ts])
+            nc.vector.tensor_tensor(
+                g_bf[a][:, ts, :].rearrange("p (c i) k -> p c k i", i=LINE),
+                part[a][:, :, ts].rearrange("p k (c i) -> p c k i", i=LINE),
+                dy[:].rearrange("p k (c i) -> p c k i", i=LINE),
+                ADD,
+            )
+
+        def quantise_g(a, t0, width):
+            ts = slice(t0, t0 + width)
+            nc.vector.quantize_mx(
+                out=g_codes[a][:, ts].bitcast(E5M2),
+                scales=g_scales[a][:, ts],
+                in_=g_bf[a][:, ts, :].rearrange("p t k -> p (t k)"),
+            )
+
+        def weights(a, h, on_vector):
+            w = sb.tile([P, PACK, HALF], F32, name=f"w{a}{h}")
+            nc.sync.dma_start(w[:], rows(wm, a)[:, :, h * HALF:(h + 1) * HALF])
+            ms = slice(h * HALF // PACK, (h + 1) * HALF // PACK)
+            dst = w_bf[a][:, :, ms, :].rearrange("p j m k -> p m k j")
+            src = w[:].rearrange("p k (m j) -> p m k j", j=PACK)
+            if on_vector:
+                nc.vector.tensor_copy(dst, src)
+            else:
+                nc.scalar.copy(dst, src)
+
+        def product(a, j):
+            cols = slice(j * P, (j + 1) * P)
+            nc.vector.quantize_mx(
+                out=w_codes[a][:, cols].bitcast(E4M3),
+                scales=w_scales[a][:, cols],
+                in_=w_bf[a][:, j, :, :].rearrange("p m k -> p (m k)"),
+            )
+            nc.tensor.matmul_mx(
+                out=banks[j][:],
+                lhsT=w_codes[a][:, cols].bitcast(E4M3),
+                lhsT_scale=w_scales[a][:, cols],
+                rhs=g_codes[a][:].bitcast(E5M2),
+                rhs_scale=g_scales[a][:],
+                start=(a == 0),
+                stop=(a == PASSES - 1),
+            )
+
+        for a in range(PASSES):
+            for k in range(PACK):
+                look_up(a, k)
+        commitment(0, 0)
+        commitment(0, 1)
+        gradient(0, 0, T)
+        quantise_g(0, 0, T)
+        commitment(1, 0)
+        commitment(1, 1)
+        weights(0, 0, False)
+        weights(0, 1, False)
+        gradient(1, 0, HALF)
+        for j in range(PACK):
+            product(0, j)
+        quantise_g(1, 0, HALF)
+        gradient(1, HALF, HALF)
+        weights(1, 0, False)
+        quantise_g(1, HALF, HALF)
+        weights(1, 1, True)
+        for j in range(PACK):
+            product(1, j)
+
+        y = sb.tile([P, PACK, T], F32, name="y")
+        y_rows = out_0.rearrange("(p j) t -> p j t", j=PACK)
+        for j in range(PACK):
+            if j % 2 == 0:
+                nc.scalar.copy(y[:, j, :], banks[j][:])
+            else:
+                nc.vector.tensor_copy(y[:, j, :], banks[j][:])
+            nc.sync.dma_start(y_rows[:, j, :], y[:, j, :])
+
+        y_bf = sb.tile([P, T, PACK], BF16, name="y_bf", align_bytes=64)
+        y_codes = sb.tile([P, T], U32, name="y_codes", align_bytes=64)
+        y_scales = sb.tile([P, T], U8, name="y_scales", align_bytes=64)
+        split = 352
+        for eng, ts in ((nc.vector.tensor_copy, slice(0, split)), (nc.scalar.copy, slice(split, T))):
+            eng(
+                y_bf[:, ts, :].rearrange("p (c i) j -> p c j i", i=LINE),
+                y[:, :, ts].rearrange("p j (c i) -> p c j i", i=LINE),
+            )
+        nc.vector.quantize_mx(
+            out=y_codes[:].bitcast(E4M3),
+            scales=y_scales[:],
+            in_=y_bf[:].rearrange("p t j -> p (t j)"),
+        )
+        nc.sync.dma_start(out_1[0].rearrange("p t j -> p (t j)").bitcast(I32), y_codes[:].bitcast(I32))
+        for q in range(4):
+            queue = nc.sync if q % 2 == 0 else nc.scalar
+            queue.dma_start(out_2[0, 4 * q:4 * q + 4, :].bitcast(I32), y_scales[32 * q:32 * q + 4, :].bitcast(I32))

@@ -14,8 +14,8 @@ U16 = mybir.dt.uint16
 U8 = mybir.dt.uint8
 E4M3 = mybir.dt.float8_e4m3fn_x4
 E5M2 = mybir.dt.float8_e5m2_x4
-MULT = mybir.AluOpType.mult
 ADD = mybir.AluOpType.add
+SUB = mybir.AluOpType.subtract
 COPY = mybir.ActivationFunctionType.Copy
 
 P = 128
@@ -23,7 +23,7 @@ PACK = 4
 K_PASS = P * PACK
 PASSES = DV // K_PASS
 HALF = 256
-LINE = 4
+LINE = 2
 
 
 def tile_attend_gvq_pl_s_x_kernel(tc, zT, cb, dyT, wm, offs, out_0, out_1, out_2):
@@ -56,12 +56,11 @@ def tile_attend_gvq_pl_s_x_kernel(tc, zT, cb, dyT, wm, offs, out_0, out_1, out_2
             nc.sync.dma_start(book[:], rows(cb, a)[:, k, :])
             nc.vector.tensor_copy(picked[a][:, k, :], book[:].indirect(offsets[:]))
 
-        def commitment(a, h):
-            ks = slice(2 * h, 2 * h + 2)
-            z = sb.tile([P, 2, T], F32, name=f"z{a}{h}")
-            nc.sync.dma_start(z[:], rows(zT, a)[:, ks, :])
-            nc.scalar.activation(zs[a][:, ks, :], z[:], COPY, scale=BETA)
-            nc.vector.scalar_tensor_tensor(part[a][:, ks, :], picked[a][:, ks, :], -BETA, zs[a][:, ks, :], MULT, ADD)
+        def commitment(a):
+            z = sb.tile([P, PACK, T], F32, name=f"z{a}")
+            nc.sync.dma_start(z[:], rows(zT, a))
+            nc.vector.tensor_tensor(zs[a][:], z[:], picked[a][:], SUB)
+            nc.scalar.activation(part[a][:], zs[a][:], COPY, scale=BETA)
 
         def gradient(a, t0, width):
             ts = slice(t0, t0 + width)
@@ -82,16 +81,16 @@ def tile_attend_gvq_pl_s_x_kernel(tc, zT, cb, dyT, wm, offs, out_0, out_1, out_2
                 in_=g_bf[a][:, ts, :].rearrange("p t k -> p (t k)"),
             )
 
-        def weights(a, h, on_vector):
-            w = sb.tile([P, PACK, HALF], F32, name=f"w{a}{h}")
-            nc.sync.dma_start(w[:], rows(wm, a)[:, :, h * HALF:(h + 1) * HALF])
-            ms = slice(h * HALF // PACK, (h + 1) * HALF // PACK)
-            dst = w_bf[a][:, :, ms, :].rearrange("p j m k -> p m k j")
-            src = w[:].rearrange("p k (m j) -> p m k j", j=PACK)
-            if on_vector:
-                nc.vector.tensor_copy(dst, src)
-            else:
-                nc.scalar.copy(dst, src)
+        def weights(a, d0, width, engines):
+            w = sb.tile([P, PACK, width], F32, name=f"w{a}{d0}")
+            nc.sync.dma_start(w[:], rows(wm, a)[:, :, d0:d0 + width])
+            ms = slice(d0 // PACK, (d0 + width) // PACK)
+            for pair, copy in enumerate(engines):
+                js = slice(2 * pair, 2 * pair + 2)
+                copy(
+                    w_bf[a][:, js, ms, :].rearrange("p j m k -> p m k j"),
+                    w[:].rearrange("p k (m j) -> p m k j", j=PACK)[:, :, :, js],
+                )
 
         def product(a, j):
             cols = slice(j * P, (j + 1) * P)
@@ -113,49 +112,52 @@ def tile_attend_gvq_pl_s_x_kernel(tc, zT, cb, dyT, wm, offs, out_0, out_1, out_2
         for a in range(PASSES):
             for k in range(PACK):
                 look_up(a, k)
-        commitment(0, 0)
-        commitment(0, 1)
+        for a in range(PASSES):
+            commitment(a)
         gradient(0, 0, T)
         quantise_g(0, 0, T)
-        commitment(1, 0)
-        commitment(1, 1)
-        weights(0, 0, False)
-        weights(0, 1, False)
+        weights(0, 0, D, (nc.scalar.copy, nc.scalar.copy))
         gradient(1, 0, HALF)
         for j in range(PACK):
             product(0, j)
-        quantise_g(1, 0, HALF)
         gradient(1, HALF, HALF)
-        weights(1, 0, False)
-        quantise_g(1, HALF, HALF)
-        weights(1, 1, True)
+        quantise_g(1, 0, T)
+        weights(1, 0, D, (nc.vector.tensor_copy, nc.scalar.copy))
         for j in range(PACK):
             product(1, j)
 
         y = sb.tile([P, PACK, T], F32, name="y")
         y_rows = out_0.rearrange("(p j) t -> p j t", j=PACK)
-        for j in range(PACK):
-            if j % 2 == 0:
-                nc.scalar.copy(y[:, j, :], banks[j][:])
-            else:
-                nc.vector.tensor_copy(y[:, j, :], banks[j][:])
+        for j, copy in enumerate((nc.scalar.copy, nc.vector.tensor_copy, nc.scalar.copy)):
+            copy(y[:, j, :], banks[j][:])
             nc.sync.dma_start(y_rows[:, j, :], y[:, j, :])
+        j = PACK - 1
+        nc.vector.tensor_copy(y[:, j, :HALF], banks[j][:, :HALF])
+        nc.scalar.copy(y[:, j, HALF:], banks[j][:, HALF:])
+        nc.sync.dma_start(y_rows[:, j, :], y[:, j, :])
 
         y_bf = sb.tile([P, T, PACK], BF16, name="y_bf", align_bytes=64)
         y_codes = sb.tile([P, T], U32, name="y_codes", align_bytes=64)
         y_scales = sb.tile([P, T], U8, name="y_scales", align_bytes=64)
-        split = 352
-        for eng, ts in ((nc.vector.tensor_copy, slice(0, split)), (nc.scalar.copy, slice(split, T))):
+        split = 384
+        for eng, ts in (
+            (nc.vector.tensor_copy, slice(0, HALF)),
+            (nc.vector.tensor_copy, slice(HALF, split)),
+            (nc.scalar.copy, slice(split, T)),
+        ):
             eng(
                 y_bf[:, ts, :].rearrange("p (c i) j -> p c j i", i=LINE),
                 y[:, :, ts].rearrange("p j (c i) -> p c j i", i=LINE),
             )
-        nc.vector.quantize_mx(
-            out=y_codes[:].bitcast(E4M3),
-            scales=y_scales[:],
-            in_=y_bf[:].rearrange("p t j -> p (t j)"),
-        )
-        nc.sync.dma_start(out_1[0].rearrange("p t j -> p (t j)").bitcast(I32), y_codes[:].bitcast(I32))
+        words = out_1[0].rearrange("p t j -> p (t j)").bitcast(I32)
+        for h in range(2):
+            ts = slice(h * HALF, (h + 1) * HALF)
+            nc.vector.quantize_mx(
+                out=y_codes[:, ts].bitcast(E4M3),
+                scales=y_scales[:, ts],
+                in_=y_bf[:, ts, :].rearrange("p t j -> p (t j)"),
+            )
+            nc.sync.dma_start(words[:, ts], y_codes[:, ts].bitcast(I32))
         for q in range(4):
-            queue = nc.sync if q % 2 == 0 else nc.scalar
+            queue = nc.sync if q % 2 == 1 else nc.scalar
             queue.dma_start(out_2[0, 4 * q:4 * q + 4, :].bitcast(I32), y_scales[32 * q:32 * q + 4, :].bitcast(I32))

@@ -16,6 +16,7 @@ E4M3 = mybir.dt.float8_e4m3fn_x4
 E5M2 = mybir.dt.float8_e5m2_x4
 ADD = mybir.AluOpType.add
 SUB = mybir.AluOpType.subtract
+MULT = mybir.AluOpType.mult
 COPY = mybir.ActivationFunctionType.Copy
 
 P = 128
@@ -24,6 +25,7 @@ K_PASS = P * PACK
 PASSES = DV // K_PASS
 HALF = 256
 LINE = 2
+RUN = 4
 
 
 def tile_attend_gvq_pl_s_x_kernel(tc, zT, cb, dyT, wm, offs, out_0, out_1, out_2):
@@ -38,11 +40,8 @@ def tile_attend_gvq_pl_s_x_kernel(tc, zT, cb, dyT, wm, offs, out_0, out_1, out_2
         psum = ctx.enter_context(tc.psum_pool(name="psum", bufs=1))
 
         offsets = held.tile([P, T // 16], U16, name="offsets")
-        nc.sync.dma_start(offsets[:], offs)
 
-        picked = [sb.tile([P, PACK, T], F32, name=f"picked{a}") for a in range(PASSES)]
-        zs = [sb.tile([P, PACK, T], F32, name=f"zs{a}") for a in range(PASSES)]
-        part = [sb.tile([P, PACK, T], F32, name=f"part{a}") for a in range(PASSES)]
+        diff = [sb.tile([P, PACK, T], F32, name=f"diff{a}") for a in range(PASSES)]
         g_bf = [sb.tile([P, T, PACK], BF16, name=f"g_bf{a}", align_bytes=64) for a in range(PASSES)]
         g_codes = [sb.tile([P, T], U32, name=f"g_codes{a}", align_bytes=64) for a in range(PASSES)]
         g_scales = [sb.tile([P, T], U8, name=f"g_scales{a}", align_bytes=64) for a in range(PASSES)]
@@ -50,47 +49,55 @@ def tile_attend_gvq_pl_s_x_kernel(tc, zT, cb, dyT, wm, offs, out_0, out_1, out_2
         w_codes = [sb.tile([P, D], U32, name=f"w_codes{a}", align_bytes=64) for a in range(PASSES)]
         w_scales = [sb.tile([P, D], U8, name=f"w_scales{a}", align_bytes=64) for a in range(PASSES)]
         banks = [psum.tile([P, T], F32, name=f"bank{j}") for j in range(PACK)]
+        sums = {}
+
+        def token_sum(a, u):
+            ks = slice(2 * u, 2 * u + 2)
+            z = sb.tile([P, 2 * T], F32, name=f"z{a}{u}")
+            dy = sb.tile([P, 2 * T], F32, name=f"dy{a}{u}")
+            nc.sync.dma_start(z[:], rows(zT, a)[:, ks, :].rearrange("p k c -> p (k c)"))
+            nc.sync.dma_start(dy[:], rows(dyT, a)[:, ks, :].rearrange("p k c -> p (k c)"))
+            sums[a, u] = sb.tile([P, 2 * T], F32, name=f"sum{a}{u}")
+            nc.vector.scalar_tensor_tensor(sums[a, u][:], dy[:], 1.0 / BETA, z[:], MULT, ADD)
 
         def look_up(a, k):
             book = sb.tile([P, C], F32, name=f"book{a}{k}")
             nc.sync.dma_start(book[:], rows(cb, a)[:, k, :])
-            nc.vector.tensor_copy(picked[a][:, k, :], book[:].indirect(offsets[:]))
+            mine = sums[a, k // 2][:, (k % 2) * T:(k % 2 + 1) * T]
+            nc.vector.tensor_tensor(diff[a][:, k, :], book[:].indirect(offsets[:]), mine, SUB)
 
-        def commitment(a):
-            z = sb.tile([P, PACK, T], F32, name=f"z{a}")
-            nc.sync.dma_start(z[:], rows(zT, a))
-            nc.vector.tensor_tensor(zs[a][:], z[:], picked[a][:], SUB)
-            nc.scalar.activation(part[a][:], zs[a][:], COPY, scale=BETA)
-
-        def gradient(a, t0, width):
-            ts = slice(t0, t0 + width)
-            dy = sb.tile([P, PACK, width], F32, name=f"dy{a}{t0}")
-            nc.sync.dma_start(dy[:], rows(dyT, a)[:, :, ts])
-            nc.vector.tensor_tensor(
-                g_bf[a][:, ts, :].rearrange("p (c i) k -> p c k i", i=LINE),
-                part[a][:, :, ts].rearrange("p k (c i) -> p c k i", i=LINE),
-                dy[:].rearrange("p k (c i) -> p c k i", i=LINE),
-                ADD,
+        def weave(tile_bf, src, ts):
+            return (
+                tile_bf[:, ts, :].rearrange("p (c i) k -> p c k i", i=RUN),
+                src[:, :, ts].rearrange("p k (c i) -> p c k i", i=RUN),
             )
 
-        def quantise_g(a, t0, width):
-            ts = slice(t0, t0 + width)
+        def gradient_scalar(a, ts):
+            dst, src = weave(g_bf[a], diff[a], ts)
+            nc.scalar.activation(dst, src, COPY, scale=-BETA)
+
+        def gradient_vector(a, ts):
+            dst, src = weave(g_bf[a], diff[a], ts)
+            nc.vector.tensor_scalar(dst, src, -BETA, None, MULT)
+
+        def quantise_g(a):
             nc.vector.quantize_mx(
-                out=g_codes[a][:, ts].bitcast(E5M2),
-                scales=g_scales[a][:, ts],
-                in_=g_bf[a][:, ts, :].rearrange("p t k -> p (t k)"),
+                out=g_codes[a][:].bitcast(E5M2),
+                scales=g_scales[a][:],
+                in_=g_bf[a][:].rearrange("p t k -> p (t k)"),
             )
 
-        def weights(a, d0, width, engines):
-            w = sb.tile([P, PACK, width], F32, name=f"w{a}{d0}")
-            nc.sync.dma_start(w[:], rows(wm, a)[:, :, d0:d0 + width])
-            ms = slice(d0 // PACK, (d0 + width) // PACK)
-            for pair, copy in enumerate(engines):
-                js = slice(2 * pair, 2 * pair + 2)
-                copy(
-                    w_bf[a][:, js, ms, :].rearrange("p j m k -> p m k j"),
-                    w[:].rearrange("p k (m j) -> p m k j", j=PACK)[:, :, :, js],
-                )
+        def load_weights(a):
+            w = sb.tile([P, PACK, D], F32, name=f"w{a}")
+            nc.sync.dma_start(w[:], rows(wm, a))
+            return w
+
+        def deal(a, w, pair, copy):
+            js = slice(2 * pair, 2 * pair + 2)
+            copy(
+                w_bf[a][:, js, :, :].rearrange("p j m k -> p m k j"),
+                w[:].rearrange("p k (m j) -> p m k j", j=PACK)[:, :, :, js],
+            )
 
         def product(a, j):
             cols = slice(j * P, (j + 1) * P)
@@ -109,20 +116,31 @@ def tile_attend_gvq_pl_s_x_kernel(tc, zT, cb, dyT, wm, offs, out_0, out_1, out_2
                 stop=(a == PASSES - 1),
             )
 
-        for a in range(PASSES):
-            for k in range(PACK):
-                look_up(a, k)
-        for a in range(PASSES):
-            commitment(a)
-        gradient(0, 0, T)
-        quantise_g(0, 0, T)
-        weights(0, 0, D, (nc.scalar.copy, nc.scalar.copy))
-        gradient(1, 0, HALF)
-        for j in range(PACK):
-            product(0, j)
-        gradient(1, HALF, HALF)
-        quantise_g(1, 0, T)
-        weights(1, 0, D, (nc.vector.tensor_copy, nc.scalar.copy))
+        token_sum(0, 0)
+        nc.sync.dma_start(offsets[:], offs)
+        look_up(0, 0)
+        look_up(0, 1)
+        token_sum(0, 1)
+        look_up(0, 2)
+        look_up(0, 3)
+        gradient_scalar(0, slice(0, T))
+        token_sum(1, 0)
+        look_up(1, 0)
+        quantise_g(0)
+        token_sum(1, 1)
+        look_up(1, 1)
+        look_up(1, 2)
+        look_up(1, 3)
+        gradient_scalar(1, slice(0, T))
+        w = load_weights(0)
+        for pair in range(2):
+            deal(0, w, pair, nc.vector.tensor_copy)
+            product(0, 2 * pair)
+            product(0, 2 * pair + 1)
+        quantise_g(1)
+        w = load_weights(1)
+        deal(1, w, 0, nc.vector.tensor_copy)
+        deal(1, w, 1, nc.scalar.copy)
         for j in range(PACK):
             product(1, j)
 

@@ -43,7 +43,7 @@ def tile_attend_gvq_pl_s_x_kernel(tc, zT, cb, dyT, wm, offs, out_0, out_1, out_2
 
         diff = [sb.tile([P, PACK, T], F32, name=f"diff{a}") for a in range(PASSES)]
         g_bf = [sb.tile([P, T, PACK], BF16, name=f"g_bf{a}", align_bytes=64) for a in range(PASSES)]
-        g_codes = [sb.tile([P, T], U32, name=f"g_codes{a}", align_bytes=64) for a in range(PASSES)]
+        g_codes = {}
         g_scales = [sb.tile([P, T], U8, name=f"g_scales{a}", align_bytes=64) for a in range(PASSES)]
         w_bf = [sb.tile([P, PACK, P, PACK], BF16, name=f"w_bf{a}", align_bytes=64) for a in range(PASSES)]
         w_codes = [sb.tile([P, D], U32, name=f"w_codes{a}", align_bytes=64) for a in range(PASSES)]
@@ -80,7 +80,8 @@ def tile_attend_gvq_pl_s_x_kernel(tc, zT, cb, dyT, wm, offs, out_0, out_1, out_2
             dst, src = weave(g_bf[a], diff[a], ts)
             nc.vector.tensor_scalar(dst, src, -BETA, None, MULT)
 
-        def quantise_g(a):
+        def quantise_g(a, slot):
+            g_codes[a] = sb.tile([P, T], U32, name=f"g_codes{a}", tag=slot, align_bytes=64)
             nc.vector.quantize_mx(
                 out=g_codes[a][:].bitcast(E5M2),
                 scales=g_scales[a][:],
@@ -88,7 +89,7 @@ def tile_attend_gvq_pl_s_x_kernel(tc, zT, cb, dyT, wm, offs, out_0, out_1, out_2
             )
 
         def load_weights(a):
-            w = sb.tile([P, PACK, D], F32, name=f"w{a}")
+            w = sb.tile([P, PACK, D], F32, name=f"w{a}", tag=f"w{a}", align_bytes=64)
             nc.sync.dma_start(w[:], rows(wm, a))
             return w
 
@@ -126,33 +127,32 @@ def tile_attend_gvq_pl_s_x_kernel(tc, zT, cb, dyT, wm, offs, out_0, out_1, out_2
         gradient_scalar(0, slice(0, T))
         token_sum(1, 0)
         look_up(1, 0)
-        quantise_g(0)
+        quantise_g(0, "g_codes")
         token_sum(1, 1)
         look_up(1, 1)
         look_up(1, 2)
         look_up(1, 3)
-        gradient_scalar(1, slice(0, T))
-        w = load_weights(0)
-        for pair in range(2):
-            deal(0, w, pair, nc.vector.tensor_copy)
-            product(0, 2 * pair)
-            product(0, 2 * pair + 1)
-        quantise_g(1)
-        w = load_weights(1)
-        deal(1, w, 0, nc.vector.tensor_copy)
-        deal(1, w, 1, nc.scalar.copy)
-        for j in range(PACK):
-            product(1, j)
+        gradient_vector(1, slice(0, 320))
+        gradient_scalar(1, slice(320, T))
+        for a in range(PASSES):
+            w = load_weights(a)
+            deal(a, w, 0, nc.vector.tensor_copy)
+            deal(a, w, 1, nc.scalar.copy)
+            for j in range(PACK):
+                if (a, j) == (0, 2):
+                    quantise_g(1, "w0")
+                product(a, j)
 
         y = sb.tile([P, PACK, T], F32, name="y")
         y_rows = out_0.rearrange("(p j) t -> p j t", j=PACK)
         for j, copy in enumerate((nc.scalar.copy, nc.vector.tensor_copy, nc.scalar.copy)):
             copy(y[:, j, :], banks[j][:])
-            nc.sync.dma_start(y_rows[:, j, :], y[:, j, :])
+            if j < 2:
+                nc.sync.dma_start(y_rows[:, j, :], y[:, j, :])
         j = PACK - 1
         nc.vector.tensor_copy(y[:, j, :HALF], banks[j][:, :HALF])
         nc.scalar.copy(y[:, j, HALF:], banks[j][:, HALF:])
-        nc.sync.dma_start(y_rows[:, j, :], y[:, j, :])
+        nc.sync.dma_start(y_rows[:, 2:, :], y[:, 2:, :])
 
         y_bf = sb.tile([P, T, PACK], BF16, name="y_bf", align_bytes=64)
         y_codes = sb.tile([P, T], U32, name="y_codes", align_bytes=64)

@@ -60,11 +60,14 @@ def tile_attend_gvq_pl_s_x_kernel(tc, zT, cb, dyT, wm, offs, out_0, out_1, out_2
             sums[a, u] = sb.tile([P, 2 * T], F32, name=f"sum{a}{u}")
             nc.vector.scalar_tensor_tensor(sums[a, u][:], dy[:], 1.0 / BETA, z[:], MULT, ADD)
 
-        def look_up(a, k):
+        def look_up(a, k, width=T):
             book = sb.tile([P, C], F32, name=f"book{a}{k}")
             nc.sync.dma_start(book[:], rows(cb, a)[:, k, :])
             mine = sums[a, k // 2][:, (k % 2) * T:(k % 2 + 1) * T]
-            nc.vector.tensor_tensor(diff[a][:, k, :], book[:].indirect(offsets[:]), mine, SUB)
+            for t0 in range(0, T, width):
+                ts = slice(t0, t0 + width)
+                codes = offsets[:, t0 // 16:(t0 + width) // 16]
+                nc.vector.tensor_tensor(diff[a][:, k, ts], book[:].indirect(codes), mine[:, ts], SUB)
 
         def weave(tile_bf, src, ts):
             return (
@@ -93,12 +96,13 @@ def tile_attend_gvq_pl_s_x_kernel(tc, zT, cb, dyT, wm, offs, out_0, out_1, out_2
             nc.sync.dma_start(w[:], rows(wm, a))
             return w
 
-        def deal(a, w, pair, copy):
+        def deal(a, w, pair, cut):
             js = slice(2 * pair, 2 * pair + 2)
-            copy(
-                w_bf[a][:, js, :, :].rearrange("p j m k -> p m k j"),
-                w[:].rearrange("p k (m j) -> p m k j", j=PACK)[:, :, :, js],
-            )
+            for copy, ms in ((nc.vector.tensor_copy, slice(0, cut)), (nc.scalar.copy, slice(cut, P))):
+                copy(
+                    w_bf[a][:, js, ms, :].rearrange("p j m k -> p m k j"),
+                    w[:].rearrange("p k (m j) -> p m k j", j=PACK)[:, ms, :, js],
+                )
 
         def product(a, j):
             cols = slice(j * P, (j + 1) * P)
@@ -131,13 +135,13 @@ def tile_attend_gvq_pl_s_x_kernel(tc, zT, cb, dyT, wm, offs, out_0, out_1, out_2
         token_sum(1, 1)
         look_up(1, 1)
         look_up(1, 2)
-        look_up(1, 3)
-        gradient_vector(1, slice(0, 320))
-        gradient_scalar(1, slice(320, T))
+        look_up(1, 3, HALF)
+        gradient_scalar(1, slice(0, HALF))
+        gradient_vector(1, slice(HALF, T))
         for a in range(PASSES):
             w = load_weights(a)
-            deal(a, w, 0, nc.vector.tensor_copy)
-            deal(a, w, 1, nc.scalar.copy)
+            deal(a, w, 0, 88)
+            deal(a, w, 1, 48)
             for j in range(PACK):
                 if (a, j) == (0, 2):
                     quantise_g(1, "w0")

@@ -155,17 +155,17 @@ def tile_attend_gvq_pl_s_x_kernel(tc, zT, cb, dyT, wm, offs, out_0, out_1, out_2
                 nc.sync.dma_start(y_rows[:, j, :], y[:, j, :])
         j = PACK - 1
         nc.vector.tensor_copy(y[:, j, :HALF], banks[j][:, :HALF])
-        nc.scalar.copy(y[:, j, HALF:], banks[j][:, HALF:])
+        nc.vector.tensor_copy(y[:, j, HALF:], banks[j][:, HALF:])
         nc.sync.dma_start(y_rows[:, 2:, :], y[:, 2:, :])
 
         y_bf = sb.tile([P, T, PACK], BF16, name="y_bf", align_bytes=64)
         y_codes = sb.tile([P, T], U32, name="y_codes", align_bytes=64)
         y_scales = sb.tile([P, T], U8, name="y_scales", align_bytes=64)
-        split = 384
         for eng, ts in (
-            (nc.vector.tensor_copy, slice(0, HALF)),
-            (nc.vector.tensor_copy, slice(HALF, split)),
-            (nc.scalar.copy, slice(split, T)),
+            (nc.vector.tensor_copy, slice(0, 160)),
+            (nc.scalar.copy, slice(160, HALF)),
+            (nc.vector.tensor_copy, slice(HALF, HALF + 160)),
+            (nc.scalar.copy, slice(HALF + 160, T)),
         ):
             eng(
                 y_bf[:, ts, :].rearrange("p (c i) j -> p c j i", i=LINE),

@@ -98,7 +98,8 @@ def tile_attend_gvq_pl_s_x_kernel(tc, zT, cb, dyT, wm, offs, out_0, out_1, out_2
 
         def deal(a, w, pair, cut):
             js = slice(2 * pair, 2 * pair + 2)
-            for copy, ms in ((nc.vector.tensor_copy, slice(0, cut)), (nc.scalar.copy, slice(cut, P))):
+            shares = ((nc.vector.tensor_copy, slice(0, cut)), (nc.scalar.copy, slice(cut, P)))
+            for copy, ms in shares[:1 if cut == P else 2]:
                 copy(
                     w_bf[a][:, js, ms, :].rearrange("p j m k -> p m k j"),
                     w[:].rearrange("p k (m j) -> p m k j", j=PACK)[:, ms, :, js],
@@ -140,7 +141,7 @@ def tile_attend_gvq_pl_s_x_kernel(tc, zT, cb, dyT, wm, offs, out_0, out_1, out_2
         gradient_vector(1, slice(HALF, T))
         for a in range(PASSES):
             w = load_weights(a)
-            deal(a, w, 0, 88)
+            deal(a, w, 0, P)
             deal(a, w, 1, 48)
             for j in range(PACK):
                 if (a, j) == (0, 2):
@@ -162,10 +163,9 @@ def tile_attend_gvq_pl_s_x_kernel(tc, zT, cb, dyT, wm, offs, out_0, out_1, out_2
         y_codes = sb.tile([P, T], U32, name="y_codes", align_bytes=64)
         y_scales = sb.tile([P, T], U8, name="y_scales", align_bytes=64)
         for eng, ts in (
-            (nc.vector.tensor_copy, slice(0, 160)),
-            (nc.scalar.copy, slice(160, HALF)),
-            (nc.vector.tensor_copy, slice(HALF, HALF + 160)),
-            (nc.scalar.copy, slice(HALF + 160, T)),
+            (nc.vector.tensor_copy, slice(0, HALF)),
+            (nc.vector.tensor_copy, slice(HALF, HALF + 128)),
+            (nc.scalar.copy, slice(HALF + 128, T)),
         ):
             eng(
                 y_bf[:, ts, :].rearrange("p (c i) j -> p c j i", i=LINE),

@@ -23,9 +23,12 @@ P = 128
 PACK = 4
 K_PASS = P * PACK
 PASSES = DV // K_PASS
-HALF = 256
+RUN = 2
 LINE = 2
-RUN = 4
+EARLY = slice(0, 384)
+EARLY_PARTS = (slice(0, 256), slice(256, 384))
+LAST = slice(384, 512)
+CUT = 48
 
 
 def tile_attend_gvq_pl_s_x_kernel(tc, zT, cb, dyT, wm, offs, out_0, out_1, out_2):
@@ -34,152 +37,172 @@ def tile_attend_gvq_pl_s_x_kernel(tc, zT, cb, dyT, wm, offs, out_0, out_1, out_2
     def rows(src, a):
         return src[a * K_PASS:(a + 1) * K_PASS, :].rearrange("(p k) c -> p k c", k=PACK)
 
+    def width(ts):
+        return ts.stop - ts.start
+
     with ExitStack() as ctx:
         held = ctx.enter_context(tc.tile_pool(name="held", bufs=1))
         sb = ctx.enter_context(tc.tile_pool(name="sb", bufs=1))
         psum = ctx.enter_context(tc.psum_pool(name="psum", bufs=1))
 
         offsets = held.tile([P, T // 16], U16, name="offsets")
-
-        diff = [sb.tile([P, PACK, T], F32, name=f"diff{a}") for a in range(PASSES)]
-        g_bf = [sb.tile([P, T, PACK], BF16, name=f"g_bf{a}", align_bytes=64) for a in range(PASSES)]
-        g_codes = {}
-        g_scales = [sb.tile([P, T], U8, name=f"g_scales{a}", align_bytes=64) for a in range(PASSES)]
-        w_bf = [sb.tile([P, PACK, P, PACK], BF16, name=f"w_bf{a}", align_bytes=64) for a in range(PASSES)]
         w_codes = [sb.tile([P, D], U32, name=f"w_codes{a}", align_bytes=64) for a in range(PASSES)]
         w_scales = [sb.tile([P, D], U8, name=f"w_scales{a}", align_bytes=64) for a in range(PASSES)]
-        banks = [psum.tile([P, T], F32, name=f"bank{j}") for j in range(PACK)]
-        sums = {}
+        commit = [sb.tile([P, PACK, T], F32, name=f"commit{a}") for a in range(PASSES)]
+        y_codes = sb.tile([P, T], U32, name="y_codes", align_bytes=64)
+        y_scales = sb.tile([P, T], U8, name="y_scales", align_bytes=64)
+        y_rows = out_0.rearrange("(p j) t -> p j t", j=PACK)
+        words = out_1[0].rearrange("p t j -> p (t j)").bitcast(I32)
+        early_banks = [psum.tile([P, width(EARLY)], F32, name=f"early{j}") for j in range(PACK)]
+        last_banks = [psum.tile([P, 2, width(LAST)], F32, name=f"last{pair}") for pair in range(2)]
 
-        def token_sum(a, u):
-            ks = slice(2 * u, 2 * u + 2)
-            z = sb.tile([P, 2 * T], F32, name=f"z{a}{u}")
-            dy = sb.tile([P, 2 * T], F32, name=f"dy{a}{u}")
-            nc.sync.dma_start(z[:], rows(zT, a)[:, ks, :].rearrange("p k c -> p (k c)"))
-            nc.sync.dma_start(dy[:], rows(dyT, a)[:, ks, :].rearrange("p k c -> p (k c)"))
-            sums[a, u] = sb.tile([P, 2 * T], F32, name=f"sum{a}{u}")
-            nc.vector.scalar_tensor_tensor(sums[a, u][:], dy[:], 1.0 / BETA, z[:], MULT, ADD)
-
-        def look_up(a, k, width=T):
-            book = sb.tile([P, C], F32, name=f"book{a}{k}")
-            nc.sync.dma_start(book[:], rows(cb, a)[:, k, :])
-            mine = sums[a, k // 2][:, (k % 2) * T:(k % 2 + 1) * T]
-            for t0 in range(0, T, width):
-                ts = slice(t0, t0 + width)
-                codes = offsets[:, t0 // 16:(t0 + width) // 16]
-                nc.vector.tensor_tensor(diff[a][:, k, ts], book[:].indirect(codes), mine[:, ts], SUB)
-
-        def weave(tile_bf, src, ts):
-            return (
-                tile_bf[:, ts, :].rearrange("p (c i) k -> p c k i", i=RUN),
-                src[:, :, ts].rearrange("p k (c i) -> p c k i", i=RUN),
-            )
-
-        def gradient_scalar(a, ts):
-            dst, src = weave(g_bf[a], diff[a], ts)
-            nc.scalar.activation(dst, src, COPY, scale=-BETA)
-
-        def gradient_vector(a, ts):
-            dst, src = weave(g_bf[a], diff[a], ts)
-            nc.vector.tensor_scalar(dst, src, -BETA, None, MULT)
-
-        def quantise_g(a, slot):
-            g_codes[a] = sb.tile([P, T], U32, name=f"g_codes{a}", tag=slot, align_bytes=64)
-            nc.vector.quantize_mx(
-                out=g_codes[a][:].bitcast(E5M2),
-                scales=g_scales[a][:],
-                in_=g_bf[a][:].rearrange("p t k -> p (t k)"),
-            )
-
-        def load_weights(a):
-            w = sb.tile([P, PACK, D], F32, name=f"w{a}", tag=f"w{a}", align_bytes=64)
+        def deal(a):
+            w = sb.tile([P, PACK, D], F32, name=f"w{a}")
             nc.sync.dma_start(w[:], rows(wm, a))
-            return w
+            dealt = []
+            shares = (
+                ((nc.vector.tensor_copy, slice(0, P)),),
+                ((nc.vector.tensor_copy, slice(0, CUT)), (nc.scalar.copy, slice(CUT, P))),
+            )
+            for pair in range(2):
+                w_bf = sb.tile([P, 2, P, PACK], BF16, name=f"w_bf{a}{pair}", tag=f"stage{a}{pair}", align_bytes=64)
+                for copy, ms in shares[pair]:
+                    copy(
+                        w_bf[:, :, ms, :].rearrange("p j m k -> p m k j"),
+                        w[:].rearrange("p k (m j) -> p m k j", j=PACK)[:, ms, :, 2 * pair:2 * pair + 2],
+                    )
+                dealt.extend([w_bf[:, 0, :, :], w_bf[:, 1, :, :]])
+            return dealt
 
-        def deal(a, w, pair, cut):
-            js = slice(2 * pair, 2 * pair + 2)
-            shares = ((nc.vector.tensor_copy, slice(0, cut)), (nc.scalar.copy, slice(cut, P)))
-            for copy, ms in shares[:1 if cut == P else 2]:
-                copy(
-                    w_bf[a][:, js, ms, :].rearrange("p j m k -> p m k j"),
-                    w[:].rearrange("p k (m j) -> p m k j", j=PACK)[:, ms, :, js],
-                )
-
-        def product(a, j):
+        def quantise_w(a, j, dealt):
             cols = slice(j * P, (j + 1) * P)
             nc.vector.quantize_mx(
                 out=w_codes[a][:, cols].bitcast(E4M3),
                 scales=w_scales[a][:, cols],
-                in_=w_bf[a][:, j, :, :].rearrange("p m k -> p (m k)"),
+                in_=dealt[j].rearrange("p m k -> p (m k)"),
             )
+
+        def load_z(a):
+            z = sb.tile([P, PACK, T], F32, name=f"z{a}")
+            nc.sync.dma_start(z[:], rows(zT, a))
+            return z
+
+        def look_up(a, k, z, step=T):
+            book = sb.tile([P, C], F32, name=f"book{a}{k}")
+            nc.sync.dma_start(book[:], rows(cb, a)[:, k, :])
+            diff = sb.tile([P, T], F32, name=f"diff{a}{k}")
+            for t0 in range(0, T, step):
+                ts = slice(t0, t0 + step)
+                codes = offsets[:, t0 // 16:(t0 + step) // 16]
+                nc.vector.tensor_tensor(diff[:, ts], book[:].indirect(codes), z[:, k, ts], SUB)
+                nc.scalar.activation(commit[a][:, k, ts], diff[:, ts], COPY, scale=-BETA)
+
+        def load_dy(a, ts):
+            dy = sb.tile([P, PACK, width(ts)], F32, name=f"dy{a}_{ts.start}")
+            nc.sync.dma_start(dy[:], rows(dyT, a)[:, :, ts])
+            return dy
+
+        def staging(a, ts):
+            return sb.tile([P, width(ts), PACK], BF16, name=f"g_bf{a}_{ts.start}", align_bytes=64)[:]
+
+        def gradient(a, ts, dy, first, g_bf):
+            nc.vector.tensor_tensor(
+                g_bf.rearrange("p (c i) k -> p c k i", i=RUN),
+                commit[a][:, :, ts].rearrange("p k (c i) -> p c k i", i=RUN),
+                dy[:, :, ts.start - first:ts.stop - first].rearrange("p k (c i) -> p c k i", i=RUN),
+                ADD,
+            )
+            return g_bf
+
+        def quantise_g(a, ts, g_bf):
+            n = width(ts)
+            codes = sb.tile([P, n], U32, name=f"g_codes{a}_{ts.start}", align_bytes=64)
+            scales = sb.tile([P, n], U8, name=f"g_scales{a}_{ts.start}", align_bytes=64)
+            nc.vector.quantize_mx(
+                out=codes[:].bitcast(E5M2),
+                scales=scales[:],
+                in_=g_bf.rearrange("p t k -> p (t k)"),
+            )
+            return codes, scales
+
+        def multiply(out, a, j, g, start, stop):
+            ds = slice(j * P, (j + 1) * P)
             nc.tensor.matmul_mx(
-                out=banks[j][:],
-                lhsT=w_codes[a][:, cols].bitcast(E4M3),
-                lhsT_scale=w_scales[a][:, cols],
-                rhs=g_codes[a][:].bitcast(E5M2),
-                rhs_scale=g_scales[a][:],
-                start=(a == 0),
-                stop=(a == PASSES - 1),
+                out=out,
+                lhsT=w_codes[a][:, ds].bitcast(E4M3),
+                lhsT_scale=w_scales[a][:, ds],
+                rhs=g[0][:].bitcast(E5M2),
+                rhs_scale=g[1][:],
+                start=start,
+                stop=stop,
             )
 
-        token_sum(0, 0)
-        nc.sync.dma_start(offsets[:], offs)
-        look_up(0, 0)
-        look_up(0, 1)
-        token_sum(0, 1)
-        look_up(0, 2)
-        look_up(0, 3)
-        gradient_scalar(0, slice(0, T))
-        token_sum(1, 0)
-        look_up(1, 0)
-        quantise_g(0, "g_codes")
-        token_sum(1, 1)
-        look_up(1, 1)
-        look_up(1, 2)
-        look_up(1, 3, HALF)
-        gradient_scalar(1, slice(0, HALF))
-        gradient_vector(1, slice(HALF, T))
-        for a in range(PASSES):
-            w = load_weights(a)
-            deal(a, w, 0, P)
-            deal(a, w, 1, 48)
+        def early_product(a, j, g):
+            for i, ts in enumerate(EARLY_PARTS):
+                multiply(early_banks[j][:, ts], a, j, g[i], a == 0 and i == 0, a == PASSES - 1 and i == 1)
+
+        def last_product(a, g):
             for j in range(PACK):
-                if (a, j) == (0, 2):
-                    quantise_g(1, "w0")
-                product(a, j)
+                multiply(last_banks[j // 2][:, j % 2, :], a, j, g, a == 0 and j % 2 == 0, a == PASSES - 1 and j % 2 == 1)
 
-        y = sb.tile([P, PACK, T], F32, name="y")
-        y_rows = out_0.rearrange("(p j) t -> p j t", j=PACK)
-        for j, copy in enumerate((nc.scalar.copy, nc.vector.tensor_copy, nc.scalar.copy)):
-            copy(y[:, j, :], banks[j][:])
-            if j < 2:
-                nc.sync.dma_start(y_rows[:, j, :], y[:, j, :])
-        j = PACK - 1
-        nc.vector.tensor_copy(y[:, j, :HALF], banks[j][:, :HALF])
-        nc.vector.tensor_copy(y[:, j, HALF:], banks[j][:, HALF:])
-        nc.sync.dma_start(y_rows[:, 2:, :], y[:, 2:, :])
-
-        y_bf = sb.tile([P, T, PACK], BF16, name="y_bf", align_bytes=64)
-        y_codes = sb.tile([P, T], U32, name="y_codes", align_bytes=64)
-        y_scales = sb.tile([P, T], U8, name="y_scales", align_bytes=64)
-        for eng, ts in (
-            (nc.vector.tensor_copy, slice(0, HALF)),
-            (nc.vector.tensor_copy, slice(HALF, HALF + 128)),
-            (nc.scalar.copy, slice(HALF + 128, T)),
-        ):
-            eng(
+        def weave_y(copy, y_bf, y, ts):
+            copy(
                 y_bf[:, ts, :].rearrange("p (c i) j -> p c j i", i=LINE),
                 y[:, :, ts].rearrange("p j (c i) -> p c j i", i=LINE),
             )
-        words = out_1[0].rearrange("p t j -> p (t j)").bitcast(I32)
-        for h in range(2):
-            ts = slice(h * HALF, (h + 1) * HALF)
+
+        def quantise_y(ts, y_bf, first):
             nc.vector.quantize_mx(
                 out=y_codes[:, ts].bitcast(E4M3),
                 scales=y_scales[:, ts],
-                in_=y_bf[:, ts, :].rearrange("p t j -> p (t j)"),
+                in_=y_bf[:, ts.start - first:ts.stop - first, :].rearrange("p t j -> p (t j)"),
             )
-            nc.sync.dma_start(words[:, ts], y_codes[:, ts].bitcast(I32))
+
+        z = load_z(0)
+        nc.sync.dma_start(offsets[:], offs)
+        for k in range(PACK):
+            look_up(0, k, z)
+        dy = load_dy(0, EARLY)
+        g_bf = [gradient(0, ts, dy, 0, staging(0, ts)) for ts in EARLY_PARTS]
+        g_first = [quantise_g(0, ts, g_bf[i]) for i, ts in enumerate(EARLY_PARTS)]
+        z = load_z(1)
+        for k in range(PACK):
+            look_up(1, k, z, T // 2 if k == PACK - 1 else T)
+        dy = load_dy(1, EARLY)
+        g_bf = [gradient(1, ts, dy, 0, staging(1, ts)) for ts in EARLY_PARTS]
+        g_second = [quantise_g(1, ts, g_bf[i]) for i, ts in enumerate(EARLY_PARTS)]
+        dealt = deal(0)
+        for j in range(PACK):
+            quantise_w(0, j, dealt)
+            early_product(0, j, g_first)
+
+        dealt = deal(1)
+        dy_last = [load_dy(a, LAST) for a in range(PASSES)]
+        y_early = sb.tile([P, PACK, width(EARLY)], F32, name="y_early")
+        for j in range(PACK):
+            quantise_w(1, j, dealt)
+            early_product(1, j, g_second)
+            nc.scalar.copy(y_early[:, j, :], early_banks[j][:])
+            nc.sync.dma_start(y_rows[:, j, EARLY], y_early[:, j, :])
+        late = sb.tile([P, PASSES, width(LAST), PACK], BF16, name="late", tag="stage10", align_bytes=64)
+        g_bf_last = [gradient(a, LAST, dy_last[a], LAST.start, late[:, a, :, :]) for a in range(PASSES)]
+        for a in range(PASSES):
+            last_product(a, quantise_g(a, LAST, g_bf_last[a]))
+
+        y_last = sb.tile([P, PACK, width(LAST)], F32, name="y_last")
+        for pair, copy in enumerate((nc.scalar.copy, nc.scalar.copy)):
+            copy(y_last[:, 2 * pair:2 * pair + 2, :], last_banks[pair][:])
+        nc.sync.dma_start(y_rows[:, :, LAST], y_last[:])
+        y_bf_early = sb.tile([P, width(EARLY), PACK], BF16, name="y_bf_early", align_bytes=64)
+        y_bf_last = sb.tile([P, width(LAST), PACK], BF16, name="y_bf_last", align_bytes=64)
+        weave_y(nc.vector.tensor_copy, y_bf_early, y_early, EARLY_PARTS[0])
+        weave_y(nc.vector.tensor_copy, y_bf_early, y_early, EARLY_PARTS[1])
+        weave_y(nc.scalar.copy, y_bf_last, y_last, slice(0, width(LAST)))
+        quantise_y(EARLY_PARTS[0], y_bf_early, 0)
+        nc.sync.dma_start(words[:, EARLY_PARTS[0]], y_codes[:, EARLY_PARTS[0]].bitcast(I32))
+        quantise_y(EARLY_PARTS[1], y_bf_early, 0)
+        quantise_y(LAST, y_bf_last, LAST.start)
+        nc.sync.dma_start(words[:, EARLY_PARTS[1].start:], y_codes[:, EARLY_PARTS[1].start:].bitcast(I32))
         for q in range(4):
             queue = nc.sync if q % 2 == 1 else nc.scalar
             queue.dma_start(out_2[0, 4 * q:4 * q + 4, :].bitcast(I32), y_scales[32 * q:32 * q + 4, :].bitcast(I32))

@@ -29,6 +29,7 @@ EARLY = slice(0, 384)
 EARLY_PARTS = (slice(0, 256), slice(256, 384))
 LAST = slice(384, 512)
 CUT = 48
+FIRST_CUT = 32
 
 
 def tile_attend_gvq_pl_s_x_kernel(tc, zT, cb, dyT, wm, offs, out_0, out_1, out_2):
@@ -56,13 +57,13 @@ def tile_attend_gvq_pl_s_x_kernel(tc, zT, cb, dyT, wm, offs, out_0, out_1, out_2
         early_banks = [psum.tile([P, width(EARLY)], F32, name=f"early{j}") for j in range(PACK)]
         last_banks = [psum.tile([P, 2, width(LAST)], F32, name=f"last{pair}") for pair in range(2)]
 
-        def deal(a):
+        def deal(a, cut):
             w = sb.tile([P, PACK, D], F32, name=f"w{a}")
             nc.sync.dma_start(w[:], rows(wm, a))
             dealt = []
             shares = (
                 ((nc.vector.tensor_copy, slice(0, P)),),
-                ((nc.vector.tensor_copy, slice(0, CUT)), (nc.scalar.copy, slice(CUT, P))),
+                ((nc.vector.tensor_copy, slice(0, cut)), (nc.scalar.copy, slice(cut, P))),
             )
             for pair in range(2):
                 w_bf = sb.tile([P, 2, P, PACK], BF16, name=f"w_bf{a}{pair}", tag=f"stage{a}{pair}", align_bytes=64)
@@ -96,6 +97,17 @@ def tile_attend_gvq_pl_s_x_kernel(tc, zT, cb, dyT, wm, offs, out_0, out_1, out_2
                 codes = offsets[:, t0 // 16:(t0 + step) // 16]
                 nc.vector.tensor_tensor(diff[:, ts], book[:].indirect(codes), z[:, k, ts], SUB)
                 nc.scalar.activation(commit[a][:, k, ts], diff[:, ts], COPY, scale=-BETA)
+
+        def load_pair(a, k):
+            book = sb.tile([P, 2 * C], F32, name=f"pair{a}{k}")
+            nc.sync.dma_start(book[:], rows(cb, a).rearrange("p k c -> p (k c)")[:, k * C:(k + 2) * C])
+            return book
+
+        def gather_pair(a, k, book, terms, scale):
+            picked = sb.tile([P, T], F32, name=f"picked{a}{k}")
+            nc.scalar.activation(terms[:, k, :], book[:].indirect(offsets[:]), COPY, scale=-BETA)
+            nc.vector.tensor_copy(picked[:], book[:, C:].indirect(offsets[:]))
+            scale(terms[:, k + 1, :], picked[:], -BETA)
 
         def load_dy(a, ts):
             dy = sb.tile([P, PACK, width(ts)], F32, name=f"dy{a}_{ts.start}")
@@ -158,25 +170,32 @@ def tile_attend_gvq_pl_s_x_kernel(tc, zT, cb, dyT, wm, offs, out_0, out_1, out_2
                 in_=y_bf[:, ts.start - first:ts.stop - first, :].rearrange("p t j -> p (t j)"),
             )
 
-        z = load_z(0)
+        terms = sb.tile([P, PACK, T], F32, name="terms")
+        later = sb.tile([P, 2, T], F32, name="later")
+        book = load_pair(0, 0)
         nc.sync.dma_start(offsets[:], offs)
-        for k in range(PACK):
-            look_up(0, k, z)
+        gather_pair(0, 0, book, terms, nc.vector.tensor_scalar_mul)
+        gather_pair(0, 2, load_pair(0, 2), terms, nc.vector.tensor_scalar_mul)
+        z = load_z(0)
+        for ts in (slice(0, T // 2), slice(T // 2, T)):
+            nc.vector.scalar_tensor_tensor(commit[0][:, :, ts], z[:, :, ts], BETA, terms[:, :, ts], MULT, ADD)
+        gather_pair(1, 0, load_pair(1, 0), later, nc.scalar.mul)
         dy = load_dy(0, EARLY)
         g_bf = [gradient(0, ts, dy, 0, staging(0, ts)) for ts in EARLY_PARTS]
         g_first = [quantise_g(0, ts, g_bf[i]) for i, ts in enumerate(EARLY_PARTS)]
         z = load_z(1)
-        for k in range(PACK):
-            look_up(1, k, z, T // 2 if k == PACK - 1 else T)
+        nc.vector.scalar_tensor_tensor(commit[1][:, 0:2, :], z[:, 0:2, :], BETA, later[:], MULT, ADD)
+        look_up(1, 2, z)
+        look_up(1, 3, z, T // 2)
         dy = load_dy(1, EARLY)
         g_bf = [gradient(1, ts, dy, 0, staging(1, ts)) for ts in EARLY_PARTS]
         g_second = [quantise_g(1, ts, g_bf[i]) for i, ts in enumerate(EARLY_PARTS)]
-        dealt = deal(0)
+        dealt = deal(0, FIRST_CUT)
         for j in range(PACK):
             quantise_w(0, j, dealt)
             early_product(0, j, g_first)
 
-        dealt = deal(1)
+        dealt = deal(1, CUT)
         dy_last = [load_dy(a, LAST) for a in range(PASSES)]
         y_early = sb.tile([P, PACK, width(EARLY)], F32, name="y_early")
         for j in range(PACK):

@@ -103,11 +103,13 @@ def tile_attend_gvq_pl_s_x_kernel(tc, zT, cb, dyT, wm, offs, out_0, out_1, out_2
             nc.sync.dma_start(book[:], rows(cb, a).rearrange("p k c -> p (k c)")[:, k * C:(k + 2) * C])
             return book
 
-        def gather_pair(a, k, book, terms, scale):
+        def gather_second(a, k, book, terms, scale):
             picked = sb.tile([P, T], F32, name=f"picked{a}{k}")
-            nc.scalar.activation(terms[:, k, :], book[:].indirect(offsets[:]), COPY, scale=-BETA)
             nc.vector.tensor_copy(picked[:], book[:, C:].indirect(offsets[:]))
             scale(terms[:, k + 1, :], picked[:], -BETA)
+
+        def gather_first(k, book, terms):
+            nc.scalar.activation(terms[:, k, :], book[:].indirect(offsets[:]), COPY, scale=-BETA)
 
         def load_dy(a, ts):
             dy = sb.tile([P, PACK, width(ts)], F32, name=f"dy{a}_{ts.start}")
@@ -174,15 +176,21 @@ def tile_attend_gvq_pl_s_x_kernel(tc, zT, cb, dyT, wm, offs, out_0, out_1, out_2
         later = sb.tile([P, 2, T], F32, name="later")
         book = load_pair(0, 0)
         nc.sync.dma_start(offsets[:], offs)
-        gather_pair(0, 0, book, terms, nc.vector.tensor_scalar_mul)
-        gather_pair(0, 2, load_pair(0, 2), terms, nc.vector.tensor_scalar_mul)
+        gather_second(0, 0, book, terms, nc.scalar.mul)
+        nc.vector.tensor_scalar(terms[:, 0, :], book[:].indirect(offsets[:]), -BETA, 0.0, MULT, ADD)
+        book = load_pair(0, 2)
+        gather_first(2, book, terms)
+        gather_second(0, 2, book, terms, nc.vector.tensor_scalar_mul)
         z = load_z(0)
         for ts in (slice(0, T // 2), slice(T // 2, T)):
             nc.vector.scalar_tensor_tensor(commit[0][:, :, ts], z[:, :, ts], BETA, terms[:, :, ts], MULT, ADD)
-        gather_pair(1, 0, load_pair(1, 0), later, nc.scalar.mul)
         dy = load_dy(0, EARLY)
         g_bf = [gradient(0, ts, dy, 0, staging(0, ts)) for ts in EARLY_PARTS]
         g_first = [quantise_g(0, ts, g_bf[i]) for i, ts in enumerate(EARLY_PARTS)]
+        for k in range(2):
+            book = sb.tile([P, C], F32, name=f"book1{k}")
+            nc.sync.dma_start(book[:], rows(cb, 1)[:, k, :])
+            gather_first(k, book, later)
         z = load_z(1)
         nc.vector.scalar_tensor_tensor(commit[1][:, 0:2, :], z[:, 0:2, :], BETA, later[:], MULT, ADD)
         look_up(1, 2, z)

@@ -224,9 +224,9 @@ def tile_attend_gvq_pl_s_x_kernel(tc, zT, cb, dyT, wm, offs, out_0, out_1, out_2
         y_bf_last = sb.tile([P, width(LAST), PACK], BF16, name="y_bf_last", align_bytes=64)
         weave_y(nc.vector.tensor_copy, y_bf_early, y_early, EARLY_PARTS[0])
         weave_y(nc.vector.tensor_copy, y_bf_early, y_early, EARLY_PARTS[1])
-        weave_y(nc.scalar.copy, y_bf_last, y_last, slice(0, width(LAST)))
         quantise_y(EARLY_PARTS[0], y_bf_early, 0)
         nc.sync.dma_start(words[:, EARLY_PARTS[0]], y_codes[:, EARLY_PARTS[0]].bitcast(I32))
+        weave_y(nc.vector.tensor_copy, y_bf_last, y_last, slice(0, width(LAST)))
         quantise_y(EARLY_PARTS[1], y_bf_early, 0)
         quantise_y(LAST, y_bf_last, LAST.start)
         nc.sync.dma_start(words[:, EARLY_PARTS[1].start:], y_codes[:, EARLY_PARTS[1].start:].bitcast(I32))

@@ -98,16 +98,6 @@ def tile_attend_gvq_pl_s_x_kernel(tc, zT, cb, dyT, wm, offs, out_0, out_1, out_2
                 nc.vector.tensor_tensor(diff[:, ts], book[:].indirect(codes), z[:, k, ts], SUB)
                 nc.scalar.activation(commit[a][:, k, ts], diff[:, ts], COPY, scale=-BETA)
 
-        def load_pair(a, k):
-            book = sb.tile([P, 2 * C], F32, name=f"pair{a}{k}")
-            nc.sync.dma_start(book[:], rows(cb, a).rearrange("p k c -> p (k c)")[:, k * C:(k + 2) * C])
-            return book
-
-        def gather_second(a, k, book, terms, scale):
-            picked = sb.tile([P, T], F32, name=f"picked{a}{k}")
-            nc.vector.tensor_copy(picked[:], book[:, C:].indirect(offsets[:]))
-            scale(terms[:, k + 1, :], picked[:], -BETA)
-
         def gather_first(k, book, terms):
             nc.scalar.activation(terms[:, k, :], book[:].indirect(offsets[:]), COPY, scale=-BETA)
 
@@ -174,16 +164,21 @@ def tile_attend_gvq_pl_s_x_kernel(tc, zT, cb, dyT, wm, offs, out_0, out_1, out_2
 
         terms = sb.tile([P, PACK, T], F32, name="terms")
         later = sb.tile([P, 2, T], F32, name="later")
-        book = load_pair(0, 0)
+        book = sb.tile([P, PACK * C], F32, name="book0")
+        nc.sync.dma_start(book[:], rows(cb, 0).rearrange("p k c -> p (k c)"))
         nc.sync.dma_start(offsets[:], offs)
-        gather_second(0, 0, book, terms, nc.scalar.mul)
-        nc.vector.tensor_scalar(terms[:, 0, :], book[:].indirect(offsets[:]), -BETA, 0.0, MULT, ADD)
-        book = load_pair(0, 2)
-        gather_first(2, book, terms)
-        gather_second(0, 2, book, terms, nc.vector.tensor_scalar_mul)
+        moved = sb.tile([P, C], F32, name="moved")
+        nc.scalar.activation(moved[:], book[:, 3 * C:], COPY)
+        picked = sb.tile([P, 2, T], F32, name="picked")
+        for k in (1, 2):
+            nc.vector.tensor_copy(picked[:, k - 1, :], book[:, k * C:(k + 1) * C].indirect(offsets[:]))
+        gather_first(0, book, terms)
+        gather_first(3, moved, terms)
+        for k in (1, 2):
+            nc.vector.tensor_scalar_mul(terms[:, k, :], picked[:, k - 1, :], -BETA)
         z = load_z(0)
-        for ts in (slice(0, T // 2), slice(T // 2, T)):
-            nc.vector.scalar_tensor_tensor(commit[0][:, :, ts], z[:, :, ts], BETA, terms[:, :, ts], MULT, ADD)
+        for ks in (slice(0, 2), slice(2, 4)):
+            nc.vector.scalar_tensor_tensor(commit[0][:, ks, :], z[:, ks, :], BETA, terms[:, ks, :], MULT, ADD)
         dy = load_dy(0, EARLY)
         g_bf = [gradient(0, ts, dy, 0, staging(0, ts)) for ts in EARLY_PARTS]
         g_first = [quantise_g(0, ts, g_bf[i]) for i, ts in enumerate(EARLY_PARTS)]
@@ -224,9 +219,9 @@ def tile_attend_gvq_pl_s_x_kernel(tc, zT, cb, dyT, wm, offs, out_0, out_1, out_2
         y_bf_last = sb.tile([P, width(LAST), PACK], BF16, name="y_bf_last", align_bytes=64)
         weave_y(nc.vector.tensor_copy, y_bf_early, y_early, EARLY_PARTS[0])
         weave_y(nc.vector.tensor_copy, y_bf_early, y_early, EARLY_PARTS[1])
+        weave_y(nc.scalar.copy, y_bf_last, y_last, slice(0, width(LAST)))
         quantise_y(EARLY_PARTS[0], y_bf_early, 0)
         nc.sync.dma_start(words[:, EARLY_PARTS[0]], y_codes[:, EARLY_PARTS[0]].bitcast(I32))
-        weave_y(nc.vector.tensor_copy, y_bf_last, y_last, slice(0, width(LAST)))
         quantise_y(EARLY_PARTS[1], y_bf_early, 0)
         quantise_y(LAST, y_bf_last, LAST.start)
         nc.sync.dma_start(words[:, EARLY_PARTS[1].start:], y_codes[:, EARLY_PARTS[1].start:].bitcast(I32))

@@ -205,7 +205,9 @@ def tile_attend_gvq_pl_s_x_kernel(tc, zT, cb, dyT, wm, offs, out_0, out_1, out_2
             quantise_w(1, j, dealt)
             early_product(1, j, g_second)
             nc.scalar.copy(y_early[:, j, :], early_banks[j][:])
-            nc.sync.dma_start(y_rows[:, j, EARLY], y_early[:, j, :])
+            if j != 2:
+                js = slice(min(j, 2), j + 1)
+                nc.sync.dma_start(y_rows[:, js, EARLY], y_early[:, js, :])
         late = sb.tile([P, PASSES, width(LAST), PACK], BF16, name="late", tag="stage10", align_bytes=64)
         g_bf_last = [gradient(a, LAST, dy_last[a], LAST.start, late[:, a, :, :]) for a in range(PASSES)]
         for a in range(PASSES):

@@ -28,6 +28,7 @@ LINE = 2
 EARLY = slice(0, 384)
 EARLY_PARTS = (slice(0, 256), slice(256, 384))
 LAST = slice(384, 512)
+SHARE = 80
 CUT = 48
 FIRST_CUT = 32
 
@@ -221,9 +222,10 @@ def tile_attend_gvq_pl_s_x_kernel(tc, zT, cb, dyT, wm, offs, out_0, out_1, out_2
         y_bf_last = sb.tile([P, width(LAST), PACK], BF16, name="y_bf_last", align_bytes=64)
         weave_y(nc.vector.tensor_copy, y_bf_early, y_early, EARLY_PARTS[0])
         weave_y(nc.vector.tensor_copy, y_bf_early, y_early, EARLY_PARTS[1])
-        weave_y(nc.scalar.copy, y_bf_last, y_last, slice(0, width(LAST)))
+        weave_y(nc.scalar.copy, y_bf_last, y_last, slice(0, SHARE))
         quantise_y(EARLY_PARTS[0], y_bf_early, 0)
         nc.sync.dma_start(words[:, EARLY_PARTS[0]], y_codes[:, EARLY_PARTS[0]].bitcast(I32))
+        weave_y(nc.vector.tensor_copy, y_bf_last, y_last, slice(SHARE, width(LAST)))
         quantise_y(EARLY_PARTS[1], y_bf_early, 0)
         quantise_y(LAST, y_bf_last, LAST.start)
         nc.sync.dma_start(words[:, EARLY_PARTS[1].start:], y_codes[:, EARLY_PARTS[1].start:].bitcast(I32))

@@ -29,8 +29,9 @@ EARLY = slice(0, 384)
 EARLY_PARTS = (slice(0, 256), slice(256, 384))
 LAST = slice(384, 512)
 SHARE = 80
-CUT = 48
-FIRST_CUT = 32
+CUTS = (96, 64)
+MOST = slice(0, 96)
+REST = slice(96, 128)
 
 
 def tile_attend_gvq_pl_s_x_kernel(tc, zT, cb, dyT, wm, offs, out_0, out_1, out_2):
@@ -58,30 +59,31 @@ def tile_attend_gvq_pl_s_x_kernel(tc, zT, cb, dyT, wm, offs, out_0, out_1, out_2
         early_banks = [psum.tile([P, width(EARLY)], F32, name=f"early{j}") for j in range(PACK)]
         last_banks = [psum.tile([P, 2, width(LAST)], F32, name=f"last{pair}") for pair in range(2)]
 
-        def deal(a, cut):
-            w = sb.tile([P, PACK, D], F32, name=f"w{a}")
-            nc.sync.dma_start(w[:], rows(wm, a))
-            dealt = []
-            shares = (
-                ((nc.vector.tensor_copy, slice(0, P)),),
-                ((nc.vector.tensor_copy, slice(0, cut)), (nc.scalar.copy, slice(cut, P))),
+        def stages(a):
+            return [
+                sb.tile([P, 2, P, PACK], BF16, name=f"w_bf{a}{pair}", tag=f"stage{a}{pair}", align_bytes=64)
+                for pair in range(2)
+            ]
+
+        def load_w(a, ms):
+            w = sb.tile([P, PACK, PACK * width(ms)], F32, name=f"w{a}_{ms.start}")
+            nc.sync.dma_start(w[:], rows(wm, a)[:, :, PACK * ms.start:PACK * ms.stop])
+            return w
+
+        def deal(copy, w_bf, w, first, pair, ms):
+            copy(
+                w_bf[pair][:, :, ms, :].rearrange("p j m k -> p m k j"),
+                w[:].rearrange("p k (m j) -> p m k j", j=PACK)[
+                    :, ms.start - first:ms.stop - first, :, 2 * pair:2 * pair + 2
+                ],
             )
-            for pair in range(2):
-                w_bf = sb.tile([P, 2, P, PACK], BF16, name=f"w_bf{a}{pair}", tag=f"stage{a}{pair}", align_bytes=64)
-                for copy, ms in shares[pair]:
-                    copy(
-                        w_bf[:, :, ms, :].rearrange("p j m k -> p m k j"),
-                        w[:].rearrange("p k (m j) -> p m k j", j=PACK)[:, ms, :, 2 * pair:2 * pair + 2],
-                    )
-                dealt.extend([w_bf[:, 0, :, :], w_bf[:, 1, :, :]])
-            return dealt
 
         def quantise_w(a, j, dealt):
             cols = slice(j * P, (j + 1) * P)
             nc.vector.quantize_mx(
                 out=w_codes[a][:, cols].bitcast(E4M3),
                 scales=w_scales[a][:, cols],
-                in_=dealt[j].rearrange("p m k -> p (m k)"),
+                in_=dealt[j // 2][:, j % 2, :, :].rearrange("p m k -> p (m k)"),
             )
 
         def load_z(a):
@@ -180,13 +182,15 @@ def tile_attend_gvq_pl_s_x_kernel(tc, zT, cb, dyT, wm, offs, out_0, out_1, out_2
         z = load_z(0)
         for ks in (slice(0, 2), slice(2, 4)):
             nc.vector.scalar_tensor_tensor(commit[0][:, ks, :], z[:, ks, :], BETA, terms[:, ks, :], MULT, ADD)
+        book = sb.tile([P, 2 * C], F32, name="book1")
+        nc.sync.dma_start(book[:], rows(cb, 1).rearrange("p k c -> p (k c)")[:, :2 * C])
+        moved = sb.tile([P, C], F32, name="moved1")
+        nc.scalar.activation(moved[:], book[:, C:], COPY)
+        gather_first(0, book, later)
+        gather_first(1, moved, later)
         dy = load_dy(0, EARLY)
         g_bf = [gradient(0, ts, dy, 0, staging(0, ts)) for ts in EARLY_PARTS]
         g_first = [quantise_g(0, ts, g_bf[i]) for i, ts in enumerate(EARLY_PARTS)]
-        for k in range(2):
-            book = sb.tile([P, C], F32, name=f"book1{k}")
-            nc.sync.dma_start(book[:], rows(cb, 1)[:, k, :])
-            gather_first(k, book, later)
         z = load_z(1)
         nc.vector.scalar_tensor_tensor(commit[1][:, 0:2, :], z[:, 0:2, :], BETA, later[:], MULT, ADD)
         look_up(1, 2, z)
@@ -194,12 +198,22 @@ def tile_attend_gvq_pl_s_x_kernel(tc, zT, cb, dyT, wm, offs, out_0, out_1, out_2
         dy = load_dy(1, EARLY)
         g_bf = [gradient(1, ts, dy, 0, staging(1, ts)) for ts in EARLY_PARTS]
         g_second = [quantise_g(1, ts, g_bf[i]) for i, ts in enumerate(EARLY_PARTS)]
-        dealt = deal(0, FIRST_CUT)
+        dealt = stages(0)
+        w = load_w(0, slice(0, P))
+        for pair in range(2):
+            deal(nc.vector.tensor_copy, dealt, w, 0, pair, slice(0, CUTS[pair]))
+            deal(nc.scalar.copy, dealt, w, 0, pair, slice(CUTS[pair], P))
         for j in range(PACK):
             quantise_w(0, j, dealt)
             early_product(0, j, g_first)
 
-        dealt = deal(1, CUT)
+        dealt = stages(1)
+        w = load_w(1, MOST)
+        deal(nc.vector.tensor_copy, dealt, w, 0, 0, MOST)
+        deal(nc.scalar.copy, dealt, w, 0, 1, MOST)
+        w = load_w(1, REST)
+        for pair in range(2):
+            deal(nc.vector.tensor_copy, dealt, w, REST.start, pair, REST)
         dy_last = [load_dy(a, LAST) for a in range(PASSES)]
         y_early = sb.tile([P, PACK, width(EARLY)], F32, name="y_early")
         for j in range(PACK):

@@ -23,6 +23,7 @@ P = 128
 PACK = 4
 K_PASS = P * PACK
 PASSES = DV // K_PASS
+BURST = 256
 RUN = 2
 LINE = 2
 EARLY = slice(0, 384)
@@ -52,8 +53,8 @@ def tile_attend_gvq_pl_s_x_kernel(tc, zT, cb, dyT, wm, offs, out_0, out_1, out_2
         w_codes = [sb.tile([P, D], U32, name=f"w_codes{a}", align_bytes=64) for a in range(PASSES)]
         w_scales = [sb.tile([P, D], U8, name=f"w_scales{a}", align_bytes=64) for a in range(PASSES)]
         commit = [sb.tile([P, PACK, T], F32, name=f"commit{a}") for a in range(PASSES)]
-        y_codes = sb.tile([P, T], U32, name="y_codes", align_bytes=64)
-        y_scales = sb.tile([P, T], U8, name="y_scales", align_bytes=64)
+        y_codes = sb.tile([P, T], U32, name="y_codes", align_bytes=BURST)
+        y_scales = sb.tile([P, T], U8, name="y_scales", align_bytes=BURST)
         y_rows = out_0.rearrange("(p j) t -> p j t", j=PACK)
         words = out_1[0].rearrange("p t j -> p (t j)").bitcast(I32)
         early_banks = [psum.tile([P, width(EARLY)], F32, name=f"early{j}") for j in range(PACK)]
@@ -66,7 +67,7 @@ def tile_attend_gvq_pl_s_x_kernel(tc, zT, cb, dyT, wm, offs, out_0, out_1, out_2
             ]
 
         def load_w(a, ms):
-            w = sb.tile([P, PACK, PACK * width(ms)], F32, name=f"w{a}_{ms.start}")
+            w = sb.tile([P, PACK, PACK * width(ms)], F32, name=f"w{a}_{ms.start}", align_bytes=BURST)
             nc.sync.dma_start(w[:], rows(wm, a)[:, :, PACK * ms.start:PACK * ms.stop])
             return w
 
@@ -87,12 +88,12 @@ def tile_attend_gvq_pl_s_x_kernel(tc, zT, cb, dyT, wm, offs, out_0, out_1, out_2
             )
 
         def load_z(a):
-            z = sb.tile([P, PACK, T], F32, name=f"z{a}")
+            z = sb.tile([P, PACK, T], F32, name=f"z{a}", align_bytes=BURST)
             nc.sync.dma_start(z[:], rows(zT, a))
             return z
 
         def look_up(a, k, z, step=T):
-            book = sb.tile([P, C], F32, name=f"book{a}{k}")
+            book = sb.tile([P, C], F32, name=f"book{a}{k}", align_bytes=BURST)
             nc.sync.dma_start(book[:], rows(cb, a)[:, k, :])
             diff = sb.tile([P, T], F32, name=f"diff{a}{k}")
             for t0 in range(0, T, step):
@@ -105,7 +106,7 @@ def tile_attend_gvq_pl_s_x_kernel(tc, zT, cb, dyT, wm, offs, out_0, out_1, out_2
             nc.scalar.activation(terms[:, k, :], book[:].indirect(offsets[:]), COPY, scale=-BETA)
 
         def load_dy(a, ts):
-            dy = sb.tile([P, PACK, width(ts)], F32, name=f"dy{a}_{ts.start}")
+            dy = sb.tile([P, PACK, width(ts)], F32, name=f"dy{a}_{ts.start}", align_bytes=BURST)
             nc.sync.dma_start(dy[:], rows(dyT, a)[:, :, ts])
             return dy
 
@@ -167,7 +168,7 @@ def tile_attend_gvq_pl_s_x_kernel(tc, zT, cb, dyT, wm, offs, out_0, out_1, out_2
 
         terms = sb.tile([P, PACK, T], F32, name="terms")
         later = sb.tile([P, 2, T], F32, name="later")
-        book = sb.tile([P, PACK * C], F32, name="book0")
+        book = sb.tile([P, PACK * C], F32, name="book0", align_bytes=BURST)
         nc.sync.dma_start(book[:], rows(cb, 0).rearrange("p k c -> p (k c)"))
         nc.sync.dma_start(offsets[:], offs)
         moved = sb.tile([P, C], F32, name="moved")
@@ -182,7 +183,7 @@ def tile_attend_gvq_pl_s_x_kernel(tc, zT, cb, dyT, wm, offs, out_0, out_1, out_2
         z = load_z(0)
         for ks in (slice(0, 2), slice(2, 4)):
             nc.vector.scalar_tensor_tensor(commit[0][:, ks, :], z[:, ks, :], BETA, terms[:, ks, :], MULT, ADD)
-        book = sb.tile([P, 2 * C], F32, name="book1")
+        book = sb.tile([P, 2 * C], F32, name="book1", align_bytes=BURST)
         nc.sync.dma_start(book[:], rows(cb, 1).rearrange("p k c -> p (k c)")[:, :2 * C])
         moved = sb.tile([P, C], F32, name="moved1")
         nc.scalar.activation(moved[:], book[:, C:], COPY)
@@ -215,7 +216,7 @@ def tile_attend_gvq_pl_s_x_kernel(tc, zT, cb, dyT, wm, offs, out_0, out_1, out_2
         for pair in range(2):
             deal(nc.vector.tensor_copy, dealt, w, REST.start, pair, REST)
         dy_last = [load_dy(a, LAST) for a in range(PASSES)]
-        y_early = sb.tile([P, PACK, width(EARLY)], F32, name="y_early")
+        y_early = sb.tile([P, PACK, width(EARLY)], F32, name="y_early", align_bytes=BURST)
         for j in range(PACK):
             quantise_w(1, j, dealt)
             early_product(1, j, g_second)
@@ -228,7 +229,7 @@ def tile_attend_gvq_pl_s_x_kernel(tc, zT, cb, dyT, wm, offs, out_0, out_1, out_2
         for a in range(PASSES):
             last_product(a, quantise_g(a, LAST, g_bf_last[a]))
 
-        y_last = sb.tile([P, PACK, width(LAST)], F32, name="y_last")
+        y_last = sb.tile([P, PACK, width(LAST)], F32, name="y_last", align_bytes=BURST)
         for pair, copy in enumerate((nc.scalar.copy, nc.scalar.copy)):
             copy(y_last[:, 2 * pair:2 * pair + 2, :], last_banks[pair][:])
         nc.sync.dma_start(y_rows[:, :, LAST], y_last[:])

@@ -29,7 +29,7 @@ LINE = 2
 EARLY = slice(0, 384)
 EARLY_PARTS = (slice(0, 256), slice(256, 384))
 LAST = slice(384, 512)
-SHARE = 80
+SHARE = 64
 CUTS = (96, 64)
 MOST = slice(0, 96)
 REST = slice(96, 128)
@@ -220,7 +220,8 @@ def tile_attend_gvq_pl_s_x_kernel(tc, zT, cb, dyT, wm, offs, out_0, out_1, out_2
         for j in range(PACK):
             quantise_w(1, j, dealt)
             early_product(1, j, g_second)
-            nc.scalar.copy(y_early[:, j, :], early_banks[j][:])
+            for ts in EARLY_PARTS if j == PACK - 1 else (EARLY,):
+                nc.scalar.copy(y_early[:, j, ts], early_banks[j][:, ts])
             if j != 2:
                 js = slice(min(j, 2), j + 1)
                 nc.sync.dma_start(y_rows[:, js, EARLY], y_early[:, js, :])
@@ -242,7 +243,8 @@ def tile_attend_gvq_pl_s_x_kernel(tc, zT, cb, dyT, wm, offs, out_0, out_1, out_2
         nc.sync.dma_start(words[:, EARLY_PARTS[0]], y_codes[:, EARLY_PARTS[0]].bitcast(I32))
         weave_y(nc.vector.tensor_copy, y_bf_last, y_last, slice(SHARE, width(LAST)))
         quantise_y(EARLY_PARTS[1], y_bf_early, 0)
-        quantise_y(LAST, y_bf_last, LAST.start)
+        quantise_y(slice(LAST.start + SHARE, LAST.stop), y_bf_last, LAST.start)
+        quantise_y(slice(LAST.start, LAST.start + SHARE), y_bf_last, LAST.start)
         nc.sync.dma_start(words[:, EARLY_PARTS[1].start:], y_codes[:, EARLY_PARTS[1].start:].bitcast(I32))
         for q in range(4):
             queue = nc.sync if q % 2 == 1 else nc.scalar

@@ -233,14 +233,14 @@ def tile_attend_gvq_pl_s_x_kernel(tc, zT, cb, dyT, wm, offs, out_0, out_1, out_2
         y_last = sb.tile([P, PACK, width(LAST)], F32, name="y_last", align_bytes=BURST)
         for pair, copy in enumerate((nc.scalar.copy, nc.scalar.copy)):
             copy(y_last[:, 2 * pair:2 * pair + 2, :], last_banks[pair][:])
-        nc.sync.dma_start(y_rows[:, :, LAST], y_last[:])
         y_bf_early = sb.tile([P, width(EARLY), PACK], BF16, name="y_bf_early", align_bytes=64)
         y_bf_last = sb.tile([P, width(LAST), PACK], BF16, name="y_bf_last", align_bytes=64)
         weave_y(nc.vector.tensor_copy, y_bf_early, y_early, EARLY_PARTS[0])
         weave_y(nc.vector.tensor_copy, y_bf_early, y_early, EARLY_PARTS[1])
         weave_y(nc.scalar.copy, y_bf_last, y_last, slice(0, SHARE))
+        nc.scalar.dma_start(y_rows[:, :, LAST], y_last[:])
         quantise_y(EARLY_PARTS[0], y_bf_early, 0)
-        nc.sync.dma_start(words[:, EARLY_PARTS[0]], y_codes[:, EARLY_PARTS[0]].bitcast(I32))
+        nc.scalar.dma_start(words[:, EARLY_PARTS[0]], y_codes[:, EARLY_PARTS[0]].bitcast(I32))
         weave_y(nc.vector.tensor_copy, y_bf_last, y_last, slice(SHARE, width(LAST)))
         quantise_y(EARLY_PARTS[1], y_bf_early, 0)
         quantise_y(slice(LAST.start + SHARE, LAST.stop), y_bf_last, LAST.start)

from contextlib import ExitStack

import concourse.mybir as mybir

T, C, D, DV = 512, 1024, 512, 1024
BETA = 0.25
FLOPS = 2 * DV * D * T

F32 = mybir.dt.float32
BF16 = mybir.dt.bfloat16
U32 = mybir.dt.uint32
I32 = mybir.dt.int32
U16 = mybir.dt.uint16
U8 = mybir.dt.uint8
E4M3 = mybir.dt.float8_e4m3fn_x4
E5M2 = mybir.dt.float8_e5m2_x4
ADD = mybir.AluOpType.add
SUB = mybir.AluOpType.subtract
MULT = mybir.AluOpType.mult
COPY = mybir.ActivationFunctionType.Copy

P = 128
PACK = 4
K_PASS = P * PACK
PASSES = DV // K_PASS
BURST = 256
RUN = 2
LINE = 2
EARLY = slice(0, 384)
EARLY_PARTS = (slice(0, 256), slice(256, 384))
LAST = slice(384, 512)
SHARE = 64
CUTS = (96, 64)
MOST = slice(0, 96)
REST = slice(96, 128)


def tile_attend_gvq_pl_s_x_kernel(tc, zT, cb, dyT, wm, offs, out_0, out_1, out_2):
    nc = tc.nc

    def rows(src, a):
        return src[a * K_PASS:(a + 1) * K_PASS, :].rearrange("(p k) c -> p k c", k=PACK)

    def width(ts):
        return ts.stop - ts.start

    with ExitStack() as ctx:
        held = ctx.enter_context(tc.tile_pool(name="held", bufs=1))
        sb = ctx.enter_context(tc.tile_pool(name="sb", bufs=1))
        psum = ctx.enter_context(tc.psum_pool(name="psum", bufs=1))

        offsets = held.tile([P, T // 16], U16, name="offsets")
        w_codes = [sb.tile([P, D], U32, name=f"w_codes{a}", align_bytes=64) for a in range(PASSES)]
        w_scales = [sb.tile([P, D], U8, name=f"w_scales{a}", align_bytes=64) for a in range(PASSES)]
        commit = [sb.tile([P, PACK, T], F32, name=f"commit{a}") for a in range(PASSES)]
        y_codes = sb.tile([P, T], U32, name="y_codes", align_bytes=BURST)
        y_scales = sb.tile([P, T], U8, name="y_scales", align_bytes=BURST)
        y_rows = out_0.rearrange("(p j) t -> p j t", j=PACK)
        words = out_1[0].rearrange("p t j -> p (t j)").bitcast(I32)
        early_banks = [psum.tile([P, width(EARLY)], F32, name=f"early{j}") for j in range(PACK)]
        last_banks = [psum.tile([P, 2, width(LAST)], F32, name=f"last{pair}") for pair in range(2)]

        def stages(a):
            return [
                sb.tile([P, 2, P, PACK], BF16, name=f"w_bf{a}{pair}", tag=f"stage{a}{pair}", align_bytes=64)
                for pair in range(2)
            ]

        def load_w(a, ms):
            w = sb.tile([P, PACK, PACK * width(ms)], F32, name=f"w{a}_{ms.start}", align_bytes=BURST)
            nc.sync.dma_start(w[:], rows(wm, a)[:, :, PACK * ms.start:PACK * ms.stop])
            return w

        def deal(copy, w_bf, w, first, pair, ms):
            copy(
                w_bf[pair][:, :, ms, :].rearrange("p j m k -> p m k j"),
                w[:].rearrange("p k (m j) -> p m k j", j=PACK)[
                    :, ms.start - first:ms.stop - first, :, 2 * pair:2 * pair + 2
                ],
            )

        def quantise_w(a, j, dealt):
            cols = slice(j * P, (j + 1) * P)
            nc.vector.quantize_mx(
                out=w_codes[a][:, cols].bitcast(E4M3),
                scales=w_scales[a][:, cols],
                in_=dealt[j // 2][:, j % 2, :, :].rearrange("p m k -> p (m k)"),
            )

        def load_z(a):
            z = sb.tile([P, PACK, T], F32, name=f"z{a}", align_bytes=BURST)
            nc.sync.dma_start(z[:], rows(zT, a))
            return z

        def look_up(a, k, z, step=T):
            book = sb.tile([P, C], F32, name=f"book{a}{k}", align_bytes=BURST)
            nc.sync.dma_start(book[:], rows(cb, a)[:, k, :])
            diff = sb.tile([P, T], F32, name=f"diff{a}{k}")
            for t0 in range(0, T, step):
                ts = slice(t0, t0 + step)
                codes = offsets[:, t0 // 16:(t0 + step) // 16]
                nc.vector.tensor_tensor(diff[:, ts], book[:].indirect(codes), z[:, k, ts], SUB)
                nc.scalar.activation(commit[a][:, k, ts], diff[:, ts], COPY, scale=-BETA)

        def gather_first(k, book, terms):
            nc.scalar.activation(terms[:, k, :], book[:].indirect(offsets[:]), COPY, scale=-BETA)

        def load_dy(a, ts):
            dy = sb.tile([P, PACK, width(ts)], F32, name=f"dy{a}_{ts.start}", align_bytes=BURST)
            nc.sync.dma_start(dy[:], rows(dyT, a)[:, :, ts])
            return dy

        def staging(a, ts):
            return sb.tile([P, width(ts), PACK], BF16, name=f"g_bf{a}_{ts.start}", align_bytes=64)[:]

        def gradient(a, ts, dy, first, g_bf):
            nc.vector.tensor_tensor(
                g_bf.rearrange("p (c i) k -> p c k i", i=RUN),
                commit[a][:, :, ts].rearrange("p k (c i) -> p c k i", i=RUN),
                dy[:, :, ts.start - first:ts.stop - first].rearrange("p k (c i) -> p c k i", i=RUN),
                ADD,
            )
            return g_bf

        def quantise_g(a, ts, g_bf):
            n = width(ts)
            codes = sb.tile([P, n], U32, name=f"g_codes{a}_{ts.start}", align_bytes=64)
            scales = sb.tile([P, n], U8, name=f"g_scales{a}_{ts.start}", align_bytes=64)
            nc.vector.quantize_mx(
                out=codes[:].bitcast(E5M2),
                scales=scales[:],
                in_=g_bf.rearrange("p t k -> p (t k)"),
            )
            return codes, scales

        def multiply(out, a, j, g, start, stop):
            ds = slice(j * P, (j + 1) * P)
            nc.tensor.matmul_mx(
                out=out,
                lhsT=w_codes[a][:, ds].bitcast(E4M3),
                lhsT_scale=w_scales[a][:, ds],
                rhs=g[0][:].bitcast(E5M2),
                rhs_scale=g[1][:],
                start=start,
                stop=stop,
            )

        def early_product(a, j, g):
            for i, ts in enumerate(EARLY_PARTS):
                multiply(early_banks[j][:, ts], a, j, g[i], a == 0 and i == 0, a == PASSES - 1 and i == 1)

        def last_product(a, g):
            for j in range(PACK):
                multiply(last_banks[j // 2][:, j % 2, :], a, j, g, a == 0 and j % 2 == 0, a == PASSES - 1 and j % 2 == 1)

        def weave_y(copy, y_bf, y, ts):
            copy(
                y_bf[:, ts, :].rearrange("p (c i) j -> p c j i", i=LINE),
                y[:, :, ts].rearrange("p j (c i) -> p c j i", i=LINE),
            )

        def quantise_y(ts, y_bf, first):
            nc.vector.quantize_mx(
                out=y_codes[:, ts].bitcast(E4M3),
                scales=y_scales[:, ts],
                in_=y_bf[:, ts.start - first:ts.stop - first, :].rearrange("p t j -> p (t j)"),
            )

        terms = sb.tile([P, PACK, T], F32, name="terms")
        later = sb.tile([P, 2, T], F32, name="later")
        book = sb.tile([P, PACK * C], F32, name="book0", align_bytes=BURST)
        nc.sync.dma_start(book[:], rows(cb, 0).rearrange("p k c -> p (k c)"))
        nc.sync.dma_start(offsets[:], offs)
        moved = sb.tile([P, C], F32, name="moved")
        nc.scalar.activation(moved[:], book[:, 3 * C:], COPY)
        picked = sb.tile([P, 2, T], F32, name="picked")
        for k in (1, 2):
            nc.vector.tensor_copy(picked[:, k - 1, :], book[:, k * C:(k + 1) * C].indirect(offsets[:]))
        gather_first(0, book, terms)
        gather_first(3, moved, terms)
        for k in (1, 2):
            nc.vector.tensor_scalar_mul(terms[:, k, :], picked[:, k - 1, :], -BETA)
        z = load_z(0)
        for ks in (slice(0, 2), slice(2, 4)):
            nc.vector.scalar_tensor_tensor(commit[0][:, ks, :], z[:, ks, :], BETA, terms[:, ks, :], MULT, ADD)
        book = sb.tile([P, 2 * C], F32, name="book1", align_bytes=BURST)
        nc.sync.dma_start(book[:], rows(cb, 1).rearrange("p k c -> p (k c)")[:, :2 * C])
        moved = sb.tile([P, C], F32, name="moved1")
        nc.scalar.activation(moved[:], book[:, C:], COPY)
        gather_first(0, book, later)
        gather_first(1, moved, later)
        dy = load_dy(0, EARLY)
        g_bf = [gradient(0, ts, dy, 0, staging(0, ts)) for ts in EARLY_PARTS]
        g_first = [quantise_g(0, ts, g_bf[i]) for i, ts in enumerate(EARLY_PARTS)]
        z = load_z(1)
        nc.vector.scalar_tensor_tensor(commit[1][:, 0:2, :], z[:, 0:2, :], BETA, later[:], MULT, ADD)
        look_up(1, 2, z)
        look_up(1, 3, z, T // 2)
        dy = load_dy(1, EARLY)
        g_bf = [gradient(1, ts, dy, 0, staging(1, ts)) for ts in EARLY_PARTS]
        g_second = [quantise_g(1, ts, g_bf[i]) for i, ts in enumerate(EARLY_PARTS)]
        dealt = stages(0)
        w = load_w(0, slice(0, P))
        for pair in range(2):
            deal(nc.vector.tensor_copy, dealt, w, 0, pair, slice(0, CUTS[pair]))
            deal(nc.scalar.copy, dealt, w, 0, pair, slice(CUTS[pair], P))
        for j in range(PACK):
            quantise_w(0, j, dealt)
            early_product(0, j, g_first)

        dealt = stages(1)
        w = load_w(1, MOST)
        deal(nc.vector.tensor_copy, dealt, w, 0, 0, MOST)
        deal(nc.scalar.copy, dealt, w, 0, 1, MOST)
        w = load_w(1, REST)
        for pair in range(2):
            deal(nc.vector.tensor_copy, dealt, w, REST.start, pair, REST)
        dy_last = [load_dy(a, LAST) for a in range(PASSES)]
        y_early = sb.tile([P, PACK, width(EARLY)], F32, name="y_early", align_bytes=BURST)
        for j in range(PACK):
            quantise_w(1, j, dealt)
            early_product(1, j, g_second)
            for ts in EARLY_PARTS if j == PACK - 1 else (EARLY,):
                nc.scalar.copy(y_early[:, j, ts], early_banks[j][:, ts])
            if j != 2:
                js = slice(min(j, 2), j + 1)
                nc.sync.dma_start(y_rows[:, js, EARLY], y_early[:, js, :])
        late = sb.tile([P, PASSES, width(LAST), PACK], BF16, name="late", tag="stage10", align_bytes=64)
        g_bf_last = [gradient(a, LAST, dy_last[a], LAST.start, late[:, a, :, :]) for a in range(PASSES)]
        for a in range(PASSES):
            last_product(a, quantise_g(a, LAST, g_bf_last[a]))

        y_last = sb.tile([P, PACK, width(LAST)], F32, name="y_last", align_bytes=BURST)
        for pair, copy in enumerate((nc.scalar.copy, nc.scalar.copy)):
            copy(y_last[:, 2 * pair:2 * pair + 2, :], last_banks[pair][:])
        y_bf_early = sb.tile([P, width(EARLY), PACK], BF16, name="y_bf_early", align_bytes=64)
        y_bf_last = sb.tile([P, width(LAST), PACK], BF16, name="y_bf_last", align_bytes=64)
        weave_y(nc.vector.tensor_copy, y_bf_early, y_early, EARLY_PARTS[0])
        weave_y(nc.vector.tensor_copy, y_bf_early, y_early, EARLY_PARTS[1])
        weave_y(nc.scalar.copy, y_bf_last, y_last, slice(0, SHARE))
        nc.scalar.dma_start(y_rows[:, :, LAST], y_last[:])
        quantise_y(EARLY_PARTS[0], y_bf_early, 0)
        nc.scalar.dma_start(words[:, EARLY_PARTS[0]], y_codes[:, EARLY_PARTS[0]].bitcast(I32))
        weave_y(nc.vector.tensor_copy, y_bf_last, y_last, slice(SHARE, width(LAST)))
        quantise_y(EARLY_PARTS[1], y_bf_early, 0)
        quantise_y(slice(LAST.start + SHARE, LAST.stop), y_bf_last, LAST.start)
        quantise_y(slice(LAST.start, LAST.start + SHARE), y_bf_last, LAST.start)
        nc.sync.dma_start(words[:, EARLY_PARTS[1].start:], y_codes[:, EARLY_PARTS[1].start:].bitcast(I32))
        for q in range(4):
            queue = nc.sync if q % 2 == 1 else nc.scalar
            queue.dma_start(out_2[0, 4 * q:4 * q + 4, :].bitcast(I32), y_scales[32 * q:32 * q + 4, :].bitcast(I32))
